import numpy as np
import ml_dtypes


def mxq(x, axis, fmt="e4m3"):
    dtype, down = {"e4m3": (ml_dtypes.float8_e4m3fn, 7), "e5m2": (ml_dtypes.float8_e5m2, 14)}[fmt]
    v = np.moveaxis(np.asarray(x, np.float32).astype(ml_dtypes.bfloat16).astype(np.float64), axis, -1)
    blocks = v.reshape(v.shape[:-1] + (-1, 32))
    amax = np.abs(blocks).max(-1, keepdims=True)
    byte = np.maximum(np.where(amax > 0, np.frexp(amax)[1] - 1 + 127, 0) - down, 1)
    scale = np.exp2(byte - 127.0)
    codes = (blocks / scale).astype(np.float32).astype(dtype).astype(np.float64)
    return np.moveaxis((codes * scale).reshape(v.shape), -1, axis)


WIDE = False


def mx_kscale(k):
    if not WIDE:
        return np.ones(k)
    levels = np.array([10, -10, 5, -5, 0])
    if k % 512:
        return np.exp2(np.random.permutation(np.resize(levels, k // 32))).repeat(32)
    a = np.empty((k // 512, 16))
    for p in range(k // 512):
        a[p, :8] = np.random.permutation(np.resize(levels, 8))
        for g in range(8):
            far = levels[np.abs(levels - a[p, g]) >= 10]
            a[p, g + 8] = far[np.random.randint(len(far))]
    return np.exp2(a.ravel()).repeat(32)


BF16 = ml_dtypes.bfloat16


def bf(x):
    return np.asarray(x, np.float32).astype(BF16)


def f64(x):
    return np.asarray(x).astype(np.float64)


E2M1 = np.array([0.0, 0.5, 1.0, 1.5, 2.0, 3.0, 4.0, 6.0, -0.0, -0.5, -1.0, -1.5, -2.0, -3.0, -4.0, -6.0])


def pack_weight(w, fmt):
    k, n = w.shape
    w = f64(bf(w)).reshape(k // 32, 32, n)
    amax = np.abs(w).max(1)
    if fmt == "e4m3":
        byte = np.frexp(amax)[1] - 1 + 127 - 7
    else:
        mant, ex = np.frexp(amax / 6.0)
        byte = np.where(mant > 0.5, ex, ex - 1) + 127
    byte = np.clip(np.where(amax > 0, byte, 1), 1, 254)
    scaled = (w * np.exp2(127.0 - byte)[:, None, :]).reshape(k, n).astype(np.float32)
    by_word = np.ascontiguousarray(scaled.reshape(k // 512, 128, 4, n).transpose(0, 1, 3, 2))
    if fmt == "e4m3":
        words = by_word.astype(ml_dtypes.float8_e4m3fn).view(np.uint8)
    else:
        c = by_word.astype(ml_dtypes.float4_e2m1fn).view(np.uint8) & 0xF
        words = c[..., 0::2] | (c[..., 1::2] << 4)
    return np.ascontiguousarray(words), np.ascontiguousarray(byte.astype(np.uint8).reshape(k // 512, 16, n))


def unpack_weight(words, scales, fmt):
    g, p, n, _ = words.shape
    if fmt == "e4m3":
        vals = np.ascontiguousarray(words).view(ml_dtypes.float8_e4m3fn).astype(np.float64)
    else:
        nib = np.empty((g, p, n, 4), np.uint8)
        nib[..., 0::2] = words & 0xF
        nib[..., 1::2] = words >> 4
        vals = E2M1[nib]
    vals = vals * np.repeat(np.exp2(scales.astype(np.float64) - 127.0), 8, axis=1)[..., None]
    return vals.transpose(0, 1, 3, 2).reshape(g * 512, n)
def pack4(w):
    words, scales = pack_weight(w, "e2m1")
    return words.reshape(words.shape[0], 128, -1), scales


def unpack4(words, scales):
    return unpack_weight(words.reshape(words.shape[0], 128, -1, 2), scales, "e2m1")


M, K, N, R = 1024, 1024, 1536, 512


def draw0():
    s, t, u = mx_kscale(K), mx_kscale(N), mx_kscale(M)
    back = np.random.standard_normal((N, K)) / np.sqrt(N) / t[:, None]
    back_words, back_scales = pack4(back)
    return {"sigma": bf(np.random.standard_normal((M, K)) * s),
            "schmid": bf(np.random.standard_normal((K, N)) / np.sqrt(K) / s[:, None]),
            "rate": bf(np.exp(0.3 * np.random.standard_normal((M, N))) * u[:, None] * t),
            "back_words": back_words,
            "back_scales": back_scales,
            "mem": bf(np.random.standard_normal((R, M)) / np.sqrt(M) / u)}


def core(sigma, schmid, rate, back_words, back_scales, mem):
    tau = mxq(f64(sigma), 1, "e4m3") @ mxq(f64(schmid), 0, "e4m3")
    slip = f64(rate) * (tau * np.abs(tau))
    strain = mxq(slip, 1, "e4m3") @ unpack4(back_words, back_scales)
    acc = mxq(f64(mem), 1, "e4m3") @ mxq(slip, 0, "e4m3")
    return strain, acc


def e4m3fn_bytes(y):
    return np.clip(np.asarray(y, np.float64), -448.0, 448.0).astype(np.float32).astype(ml_dtypes.float8_e4m3fn).view(np.uint8)


def e4m3fn_values(b):
    return np.asarray(b, np.uint8).view(ml_dtypes.float8_e4m3fn).astype(np.float64)


def setup_inputs():
    d = draw0()
    x0 = np.asarray(d['schmid']).astype(np.float64)
    s = (np.max(np.abs(x0), axis=(1,), keepdims=True) / 448.0).astype(np.float32)
    out = {}
    for k, v in d.items():
        if k == 'schmid':
            out['schmid_bytes'] = e4m3fn_bytes(x0 / s.astype(np.float64))
            out['schmid_scale'] = s
        else:
            out[k] = v
    return out


def reference(sigma, schmid_bytes, schmid_scale, rate, back_words, back_scales, mem):
    return core(sigma, e4m3fn_values(schmid_bytes) * schmid_scale.astype(np.float64), rate, back_words, back_scales, mem)

@@ -1,0 +1,475 @@
+from contextlib import ExitStack
+
+import concourse.mybir as mybir
+from concourse.masks import make_identity
+
+F32 = mybir.dt.float32
+BF16 = mybir.dt.bfloat16
+U32 = mybir.dt.uint32
+I32 = mybir.dt.int32
+U8 = mybir.dt.uint8
+FP8 = mybir.dt.float8_e4m3fn
+FP8X4 = mybir.dt.float8_e4m3fn_x4
+FP4X4 = mybir.dt.float4_e2m1fn_x4
+MULT = mybir.AluOpType.mult
+ABS = mybir.ActivationFunctionType.Abs
+COPY = mybir.ActivationFunctionType.Copy
+
+M, K, N, R, C = 1024, 1024, 1536, 512, 1024
+FLOPS = 2 * (M * K * N + M * N * C + R * M * N)
+P = 128
+B = 512
+
+MANUAL = True
+
+
+def tile_crystal_slip_rates_s8_kernel(
+    tc, sigma, schmid_bytes, schmid_scale, rate, back_words, back_scales, mem, strain, acc
+):
+    nc = tc.nc
+    S, V, PE = nc.scalar, nc.vector, nc.tensor
+    with ExitStack() as ctx:
+        keep = ctx.enter_context(tc.tile_pool(name="keep", bufs=1))
+        work = ctx.enter_context(tc.tile_pool(name="work", bufs=2))
+        psum = ctx.enter_context(tc.psum_pool(name="psum", bufs=1))
+
+        ident = keep.tile([P, P], F32, name="ident")
+        warm = keep.tile([P, 8], F32, name="warm")
+        scl = keep.tile([P, 2, 4], F32, name="scl")
+        byt0 = keep.tile([P, 2, 4, 512], U8, name="byt0")
+        byt1 = keep.tile([P, 2, 4, 1024], U8, name="byt1")
+        rate_sb = keep.tile([P, 2, 4, N], BF16, name="rate_sb")
+        sig_codes = keep.tile([P, 2, 2, B], U32, name="sig_codes", align_bytes=64)
+        sig_sc = keep.tile([P, 2, 2, B], U8, name="sig_sc", align_bytes=64)
+        sch_codes = keep.tile([P, 2, N], U32, name="sch_codes", align_bytes=64)
+        sch_sc = keep.tile([P, 2, N], U8, name="sch_sc", align_bytes=64)
+        mem_codes = keep.tile([P, 2, B], U32, name="mem_codes", align_bytes=64)
+        mem_sc = keep.tile([P, 2, B], U8, name="mem_sc", align_bytes=64)
+        row_codes = keep.tile([P, 2, N], U32, name="row_codes", align_bytes=64)
+        row_sc = keep.tile([P, 2, N], U8, name="row_sc", align_bytes=64)
+        col_codes = keep.tile([P, 2, 3, B], U32, name="col_codes", align_bytes=64)
+        col_sc = keep.tile([P, 2, 3, B], U8, name="col_sc", align_bytes=64)
+        bw = keep.tile([P, 3, 2 * C], U8, name="bw", align_bytes=64)
+        bsc = keep.tile([P, 3, C], U8, name="bsc", align_bytes=64)
+
+        V.memset(warm[:], 0.0)
+        S.activation(out=warm[:, 1:2], in_=warm[:, 0:1], func=ABS)
+        make_identity(nc, ident[:])
+        nc.gpsimd.memset(bsc[:].rearrange("p g n -> p (g n)").bitcast(I32), 0)
+
+        raw = {}
+        nc.sync.dma_start(out=scl[:], in_=schmid_scale.rearrange("(g p t) o -> p g (t o)", p=P, t=4))
+
+        def load_rows(key, src, h, parts=2):
+            raw[key] = work.tile([P, 4, 1024], BF16, name="raw", tag="raw", bufs=3, align_bytes=64)
+            v = src[h * B : (h + 1) * B, :].rearrange("(p t) k -> p t k", t=4)
+            w = 4 // parts
+            for j in range(parts):
+                nc.sync.dma_start(out=raw[key][:, w * j : w * j + w, :], in_=v[:, w * j : w * j + w, :])
+
+        def load_bytes(g, rest):
+            v = schmid_bytes[g * B : (g + 1) * B, :].rearrange("(p t) n -> p t n", t=4)
+            if rest:
+                nc.sync.dma_start(out=byt1[:, g], in_=v[:, :, 512:])
+            else:
+                nc.sync.dma_start(out=byt0[:, g], in_=v[:, :, 0:512])
+
+        def load_rate(h, n0, n1):
+            nc.sync.dma_start(
+                out=rate_sb[:, h, :, n0:n1], in_=rate[h * B : (h + 1) * B, n0:n1].rearrange("(p t) n -> p t n", t=4)
+            )
+
+        load_bytes(0, False)
+        load_bytes(1, False)
+        load_rows("s0", sigma, 0)
+        load_bytes(0, True)
+        load_rate(0, 0, 512)
+        load_bytes(1, True)
+        load_rate(0, 512, N)
+        load_rows("s1", sigma, 1)
+        load_rows("m", mem, 0, parts=1)
+        load_rate(1, 0, N)
+        nc.sync.dma_start(
+            out=bw[:].bitcast(I32), in_=back_words.rearrange("g p w -> p g w").bitcast(I32)
+        )
+        for q in range(4):
+            nc.sync.dma_start(
+                out=bsc[32 * q : 32 * q + 4].bitcast(I32),
+                in_=back_scales[:, 4 * q : 4 * q + 4, :].rearrange("g q n -> q g n").bitcast(I32),
+            )
+
+        def copy(eng, out, in_):
+            if eng is S:
+                S.copy(out=out, in_=in_)
+            else:
+                V.tensor_copy(out=out, in_=in_)
+
+        grp = {}
+
+        def new_grp(key):
+            grp[key] = work.tile([P, B, 4], BF16, name="grp", tag="grp", bufs=4, align_bytes=64)
+
+        def bank(tag, shape):
+            return psum.tile(shape, F32, name=tag, tag=tag, bufs={"tau": 4, "out": 3, "tr": 1}[tag])
+
+        def turn(key, src, wbase, t0, eng, tag="tr", off=0, step=2):
+            tr = bank(tag, [P, 2, 2, P])
+            for a in range(2):
+                words = src[:, t0 + a, :].bitcast(F32)
+                for u in range(2):
+                    w = words[:, wbase + u : wbase + 256 : 2] if step == 2 else words[:, u * P : (u + 1) * P]
+                    PE.transpose(tr[:, a, u, :], w, ident[:])
+            dst = grp[key][:, (t0 - off) * P : (t0 - off + 2) * P, :].bitcast(F32)
+            copy(
+                eng,
+                dst.rearrange("p (a r) u -> p a r u", a=2),
+                tr[:].rearrange("p a u r -> p a r u"),
+            )
+
+        def quant(key, codes, scales, c0=0, c1=B):
+            V.quantize_mx(
+                out=codes.bitcast(FP8X4),
+                scales=scales,
+                in_=grp[key][:, c0:c1, :].rearrange("p c t -> p (c t)"),
+            )
+
+        def sig_turn(h, g, t0, eng, tag="tr"):
+            key = ("sig", h, g)
+            if t0 == 0:
+                new_grp(key)
+            turn(key, raw["s%d" % h], 256 * g, t0, eng, tag)
+
+        def sig_quant(h, g):
+            quant(("sig", h, g), sig_codes[:, h, g, :], sig_sc[:, h, g, :])
+
+        def mem_turn(g, t0, eng, tag="tr"):
+            key = ("mem", g)
+            if t0 == 0:
+                new_grp(key)
+            turn(key, raw["m"], 256 * g, t0, eng, tag)
+
+        def mem_quant(g):
+            quant(("mem", g), mem_codes[:, g, :], mem_sc[:, g, :])
+
+        wide = {}
+
+        def widen(g, nb, ts, eng):
+            key = (g, nb)
+            if key not in wide:
+                wide[key] = work.tile([P, 4, B], BF16, name="wide", tag="wide", bufs=3, align_bytes=64)
+            for t in ts:
+                b = byt0[:, g, t, :] if nb == 0 else byt1[:, g, t, (nb - 1) * B : nb * B]
+                b = b.bitcast(FP8)
+                s = scl[:, g, t : t + 1]
+                if eng is S:
+                    S.activation(out=wide[key][:, t, :], in_=b, func=COPY, scale=s)
+                else:
+                    V.tensor_scalar(out=wide[key][:, t, :], in0=b, scalar1=s, scalar2=None, op0=MULT)
+
+        def sch_inter(g, nb, eng):
+            key = ("sch", g, nb)
+            new_grp(key)
+            copy(eng, grp[key][:], wide[(g, nb)][:].rearrange("p t n -> p n t"))
+
+        def sch_quant(g, nb):
+            c = slice(nb * B, nb * B + B)
+            quant(("sch", g, nb), sch_codes[:, g, c], sch_sc[:, g, c])
+
+        tau, w_sb, a_sb, slip = {}, {}, {}, {}
+
+        def mm(out, lc, ls, rc, rs, start, stop, fp4=False):
+            PE.matmul_mx(
+                out=out,
+                lhsT=lc.bitcast(FP8X4),
+                lhsT_scale=ls,
+                rhs=rc.bitcast(FP4X4 if fp4 else FP8X4),
+                rhs_scale=rs,
+                start=start,
+                stop=stop,
+            )
+
+        def do_tau(i, t):
+            h, nb = units[i]
+            ps = psum.tile([P, B], F32, name="tau", tag="tau", bufs=4)
+            c, n = slice(t * P, t * P + P), slice(nb * B, nb * B + B)
+            for g in range(2):
+                mm(ps[:], sig_codes[:, h, g, c], sig_sc[:, h, g, c], sch_codes[:, g, n], sch_sc[:, g, n], g == 0, g == 1)
+            tau[(i, t)] = ps
+
+        def half(d, i, t, name, dt, bufs):
+            key = (i, t // 2)
+            if key not in d:
+                d[key] = work.tile([P, 2, B], dt, name=name, tag=name, bufs=bufs)
+            return d[key]
+
+        def ab(i, t):
+            a = half(a_sb, i, t, "a_sb", F32, 3)
+            S.activation(out=a[:, t % 2, :], in_=tau[(i, t)][:], func=ABS)
+
+        def v1(i, t):
+            h, nb = units[i]
+            w = half(w_sb, i, t, "w_sb", F32, 3)
+            V.tensor_tensor(
+                out=w[:, t % 2, :], in0=tau[(i, t)][:], in1=rate_sb[:, h, t, nb * B : nb * B + B], op=MULT
+            )
+
+        def prod(i, t0):
+            if i not in slip:
+                slip[i] = work.tile([P, 4, B], BF16, name="slip", tag="slip", bufs=4, align_bytes=64)
+            for t in (t0, t0 + 1):
+                V.tensor_tensor(
+                    out=slip[i][:, t, :].rearrange("p (u i e) -> p u i e", u=2, e=2),
+                    in0=w_sb[(i, t0 // 2)][:, t % 2, :].rearrange("p (i u e) -> p u i e", u=2, e=2),
+                    in1=a_sb[(i, t0 // 2)][:, t % 2, :].rearrange("p (i u e) -> p u i e", u=2, e=2),
+                    op=MULT,
+                )
+
+        def slip_turn(i, t0, eng, tag="tr"):
+            key = ("col", i, t0)
+            grp[key] = work.tile([P, 2 * P, 4], BF16, name="colgrp", tag="colgrp", bufs=4, align_bytes=64)
+            turn(key, slip[i], 0, t0, eng, tag, t0, 1)
+
+        def col_quant(i, t0):
+            h, nb = units[i]
+            c = slice(t0 * P, (t0 + 2) * P)
+            quant(("col", i, t0), col_codes[:, h, nb, c], col_sc[:, h, nb, c], 0, 2 * P)
+
+        def row_inter(i, eng=V, c0=0, c1=B):
+            key = ("row", i)
+            if c0 == 0:
+                new_grp(key)
+            copy(eng, grp[key][:, c0:c1, :], slip[i][:, :, c0:c1].rearrange("p t n -> p n t"))
+
+        def row_quant(i, c0=0, c1=B):
+            h, nb = units[i]
+            n = slice(nb * B + c0, nb * B + c1)
+            quant(("row", i), row_codes[:, h, n], row_sc[:, h, n], c0, c1)
+
+        strain_v = strain.rearrange("(h p t) c -> h p t c", p=P, t=4)
+        acc_v = acc.rearrange("(p s) n -> p s n", s=4)
+        st2, osb = {}, {}
+
+        def st2_mm(h, t, c, gs, tag="out"):
+            key = (h, t, c)
+            if key not in st2:
+                nbufs = {"out": 3, "tau": 4, "tr": 1}[tag]
+                st2[key] = psum.tile([P, B], F32, name=tag, tag=tag, bufs=nbufs)
+            m = slice(t * P, t * P + P)
+            for g in gs:
+                mm(
+                    st2[key][:],
+                    col_codes[:, h, g, m],
+                    col_sc[:, h, g, m],
+                    bw[:, g, 2 * c * B : 2 * (c + 1) * B],
+                    bsc[:, g, c * B : (c + 1) * B],
+                    g == 0,
+                    g == 2,
+                    fp4=True,
+                )
+
+        def st2_out(h, t, c, eng):
+            if c == 0:
+                osb[(h, t)] = work.tile([P, C], F32, name="osb", tag="osb", bufs=3)
+            o = osb[(h, t)]
+            copy(eng, o[:, c * B : (c + 1) * B], st2[(h, t, c)][:])
+            if c == 1:
+                nc.sync.dma_start(out=strain_v[h, :, t, :], in_=o[:])
+
+        def st2_full(h, t, c, eng, tag="out"):
+            st2_mm(h, t, c, range(3), tag)
+            st2_out(h, t, c, eng)
+
+        st3, oacc = {}, {}
+
+        def st3_mm(nb, s, c0=0, c1=B, tag="out"):
+            key = (nb, s)
+            if c0 == 0:
+                nbufs = {"out": 3, "tau": 4, "tr": 1}[tag]
+                st3[key] = psum.tile([P, B], F32, name=tag, tag=tag, bufs=nbufs)
+            m, n = slice(s * P, s * P + P), slice(nb * B + c0, nb * B + c1)
+            for h in range(2):
+                mm(st3[key][:, c0:c1], mem_codes[:, h, m], mem_sc[:, h, m], row_codes[:, h, n], row_sc[:, h, n], h == 0, h == 1)
+
+        def st3_out(nb, s, eng):
+            o = work.tile([P, B], F32, name="oacc", tag="oacc", bufs=5)
+            copy(
+                eng,
+                o[:].rearrange("p (i u e) -> p i u e", u=2, e=2),
+                st3[(nb, s)][:].rearrange("p (u i e) -> p i u e", u=2, e=2),
+            )
+            nc.sync.dma_start(out=acc_v[:, s, nb * B : nb * B + B], in_=o[:])
+
+        def st3_full(nb, s, eng, tag="out"):
+            st3_mm(nb, s, tag=tag)
+            st3_out(nb, s, eng)
+
+        units = [(0, 0), (0, 1), (0, 2), (1, 0), (1, 1), (1, 2)]
+
+        if MANUAL:
+            ctx.enter_context(
+                tc.manual_schedule(
+                    engines={mybir.EngineType.PE, mybir.EngineType.Activation, mybir.EngineType.DVE}
+                )
+            )
+
+        widen(0, 0, (0,), S)
+        widen(0, 0, (1, 2, 3), V)
+        widen(1, 0, (0,1), S)
+        sch_inter(0, 0, V)
+        widen(1, 0, (2, 3), V)
+        sch_quant(0, 0)
+        sig_turn(0, 0, 0, S)
+        sig_turn(0, 1, 0, S, "out")
+        sch_inter(1, 0, V)
+        sig_turn(0, 0, 2, S, "out")
+        sig_turn(0, 1, 2, S, "out")
+        sch_quant(1, 0)
+        sig_quant(0, 0)
+        sig_quant(0, 1)
+
+        L = lambda f, *a: (lambda: f(*a))
+
+        def run(fs):
+            for f in fs:
+                f()
+
+        for t in range(4):
+            do_tau(0, t)
+        widen(0, 1, range(4), S)
+        for t in range(4):
+            v1(0, t)
+            ab(0, t)
+
+        prod(0, 0)
+        slip_turn(0, 0, S)
+        prod(0, 2)
+        widen(1, 1, range(2), S)
+        slip_turn(0, 2, S, "out")
+        sch_inter(0, 1, V)
+        widen(1, 1, range(2, 4), S)
+        row_inter(0)
+        sch_quant(0, 1)
+        sch_inter(1, 1, V)
+        widen(0, 2, range(4), S)
+        col_quant(0, 0)
+        col_quant(0, 2)
+        sch_quant(1, 1)
+        for t in range(4):
+            do_tau(1, t)
+        row_quant(0)
+        sch_inter(0, 2, S)
+        for t in range(4):
+            v1(1, t)
+            ab(1, t)
+        widen(1, 2, range(4), S)
+        sch_quant(0, 2)
+        prod(1, 0)
+        slip_turn(1, 0, S)
+        prod(1, 2)
+        slip_turn(1, 2, S, "out")
+        row_inter(1)
+        sch_inter(1, 2, V)
+        sig_turn(1, 0, 0, S)
+        sig_turn(1, 1, 0, S, "out")
+        sig_turn(1, 0, 2, S, "out")
+        sig_turn(1, 1, 2, S, "out")
+        col_quant(1, 0)
+        col_quant(1, 2)
+        sch_quant(1, 2)
+        mem_fill = [L(mem_turn, 0, 0, S), L(mem_turn, 1, 0, S, "out"), L(mem_turn, 0, 2, S, "out"), L(mem_turn, 1, 2, S, "out")]
+        run(mem_fill[:2])
+        for t in range(4):
+            do_tau(2, t)
+        row_quant(1)
+        sig_quant(1, 0)
+        v1(2, 0)
+        v1(2, 1)
+        ab(2, 0)
+        ab(2, 1)
+        sig_quant(1, 1)
+
+        st2a = [L(st2_full, 0, t, c, S) for t in range(2) for c in range(2)]
+        st2b = [L(st2_full, 0, t, c, S) for t in range(2, 4) for c in range(2)]
+        st2c = [L(st2_full, 1, t, c, S) for t in range(2) for c in range(2)]
+        st3a = [L(st3_full, 0, s, S) for s in range(4)]
+        st3b = [L(st3_full, 1, s, S) for s in range(4)]
+
+        halves = [(2, 0), (2, 2), (3, 0), (4, 0), (5, 0), (3, 2), (4, 2), (5, 2)]
+
+        def front(k):
+            i, t0 = halves[k]
+            for t in (t0, t0 + 1):
+                v1(i, t)
+                if k + 2 < len(halves):
+                    do_tau(halves[k + 2][0], halves[k + 2][1] + t - t0)
+
+        def absk(k):
+            if k < len(halves):
+                i, t0 = halves[k]
+                ab(i, t0)
+                ab(i, t0 + 1)
+
+        def back(k, fill):
+            i, t0 = halves[k]
+            prod(i, t0)
+            absk(k + 1)
+            slip_turn(i, t0, S)
+            run(fill)
+
+        def cq(k):
+            col_quant(*halves[k])
+
+        do_tau(3, 0)
+        do_tau(3, 1)
+        back(0, mem_fill[2:])
+        front(1)
+        cq(0)
+        back(1, st2a)
+        row_inter(2)
+        mem_quant(0)
+        front(2)
+        cq(1)
+        row_quant(2)
+        back(2, st2b[:2])
+        front(3)
+        cq(2)
+        back(3, st2b[2:])
+        mem_quant(1)
+        front(4)
+        cq(3)
+        back(4, [])
+        front(5)
+        cq(4)
+        back(5, st2c)
+        row_inter(3)
+        front(6)
+        cq(5)
+        row_quant(3)
+        back(6, st3a)
+        row_inter(4)
+        front(7)
+        cq(6)
+        row_quant(4)
+        for t in range(2, 4):
+            for c in range(2):
+                st2_mm(1, t, c, range(2), "tau")
+        prod(5, 2)
+        slip_turn(5, 2, S)
+        row_inter(5, V, 0, 256)
+        run(st3b)
+        col_quant(5, 2)
+        row_quant(5, 0, 256)
+        row_inter(5, V, 256, 512)
+        for t in range(2, 4):
+            for c in range(2):
+                st2_mm(1, t, c, (2,), "tau")
+        for t in range(2, 4):
+            for c in range(2):
+                st2_out(1, t, c, (S, V)[c])
+        for s in range(4):
+            st3_mm(2, s, 0, 256, ("out", "out", "out", "tr")[s])
+        row_quant(5, 256, 512)
+        for s in range(4):
+            st3_mm(2, s, 256, 512)
+        for s in range(4):
+            st3_out(2, s, (S, V)[s % 2])

@@ -19,8 +19,7 @@ M, K, N, R, C = 1024, 1024, 1536, 512, 1024
 FLOPS = 2 * (M * K * N + M * N * C + R * M * N)
 P = 128
 B = 512
-
-MANUAL = True
+BANKS = {"A": 4, "B": 3, "C": 1}
 
 
 def tile_crystal_slip_rates_s8_kernel(
@@ -34,10 +33,11 @@ def tile_crystal_slip_rates_s8_kernel(
         psum = ctx.enter_context(tc.psum_pool(name="psum", bufs=1))
 
         ident = keep.tile([P, P], F32, name="ident")
-        warm = keep.tile([P, 8], F32, name="warm")
+        touch = keep.tile([P, 8], F32, name="touch")
+        zb = keep.tile([P, B], BF16, name="zb")
         scl = keep.tile([P, 2, 4], F32, name="scl")
-        byt0 = keep.tile([P, 2, 4, 512], U8, name="byt0")
-        byt1 = keep.tile([P, 2, 4, 1024], U8, name="byt1")
+        byt0 = keep.tile([P, 2, 4, B], U8, name="byt0")
+        byt1 = keep.tile([P, 2, 4, 2 * B], U8, name="byt1")
         rate_sb = keep.tile([P, 2, 4, N], BF16, name="rate_sb")
         sig_codes = keep.tile([P, 2, 2, B], U32, name="sig_codes", align_bytes=64)
         sig_sc = keep.tile([P, 2, 2, B], U8, name="sig_sc", align_bytes=64)
@@ -52,51 +52,44 @@ def tile_crystal_slip_rates_s8_kernel(
         bw = keep.tile([P, 3, 2 * C], U8, name="bw", align_bytes=64)
         bsc = keep.tile([P, 3, C], U8, name="bsc", align_bytes=64)
 
-        V.memset(warm[:], 0.0)
-        S.activation(out=warm[:, 1:2], in_=warm[:, 0:1], func=ABS)
+        V.memset(zb[:], 0.0)
+        V.memset(touch[:], 0.0)
+        S.activation(out=touch[:, 1:2], in_=touch[:, 0:1], func=ABS)
         make_identity(nc, ident[:])
         nc.gpsimd.memset(bsc[:].rearrange("p g n -> p (g n)").bitcast(I32), 0)
 
         raw = {}
-        nc.sync.dma_start(out=scl[:], in_=schmid_scale.rearrange("(g p t) o -> p g (t o)", p=P, t=4))
 
-        def load_rows(key, src, h, parts=2):
-            raw[key] = work.tile([P, 4, 1024], BF16, name="raw", tag="raw", bufs=3, align_bytes=64)
-            v = src[h * B : (h + 1) * B, :].rearrange("(p t) k -> p t k", t=4)
-            w = 4 // parts
-            for j in range(parts):
-                nc.sync.dma_start(out=raw[key][:, w * j : w * j + w, :], in_=v[:, w * j : w * j + w, :])
+        def load_rows(key, src, t0):
+            raw[key] = work.tile([P, 2, 1024], BF16, name="raw", tag="raw", bufs=4, align_bytes=64)
+            v = src.rearrange("(p t) k -> p t k", t=4)
+            nc.sync.dma_start(out=raw[key][:], in_=v[:, t0 : t0 + 2, :])
+
+        def load_sigma(h, t0):
+            load_rows(("s", h, t0), sigma[h * B : (h + 1) * B, :], t0)
 
         def load_bytes(g, rest):
             v = schmid_bytes[g * B : (g + 1) * B, :].rearrange("(p t) n -> p t n", t=4)
             if rest:
-                nc.sync.dma_start(out=byt1[:, g], in_=v[:, :, 512:])
+                nc.sync.dma_start(out=byt1[:, g], in_=v[:, :, B:])
             else:
-                nc.sync.dma_start(out=byt0[:, g], in_=v[:, :, 0:512])
+                nc.sync.dma_start(out=byt0[:, g], in_=v[:, :, 0:B])
 
         def load_rate(h, n0, n1):
             nc.sync.dma_start(
                 out=rate_sb[:, h, :, n0:n1], in_=rate[h * B : (h + 1) * B, n0:n1].rearrange("(p t) n -> p t n", t=4)
             )
 
-        load_bytes(0, False)
-        load_bytes(1, False)
-        load_rows("s0", sigma, 0)
-        load_bytes(0, True)
-        load_rate(0, 0, 512)
-        load_bytes(1, True)
-        load_rate(0, 512, N)
-        load_rows("s1", sigma, 1)
-        load_rows("m", mem, 0, parts=1)
-        load_rate(1, 0, N)
-        nc.sync.dma_start(
-            out=bw[:].bitcast(I32), in_=back_words.rearrange("g p w -> p g w").bitcast(I32)
-        )
-        for q in range(4):
-            nc.sync.dma_start(
-                out=bsc[32 * q : 32 * q + 4].bitcast(I32),
-                in_=back_scales[:, 4 * q : 4 * q + 4, :].rearrange("g q n -> q g n").bitcast(I32),
-            )
+        def load_back():
+            nc.sync.dma_start(out=bw[:].bitcast(I32), in_=back_words.rearrange("g p w -> p g w").bitcast(I32))
+            for q in range(4):
+                nc.sync.dma_start(
+                    out=bsc[32 * q : 32 * q + 4].bitcast(I32),
+                    in_=back_scales[:, 4 * q : 4 * q + 4, :].rearrange("g q n -> q g n").bitcast(I32),
+                )
+
+        def load_scale():
+            nc.sync.dma_start(out=scl[:], in_=schmid_scale.rearrange("(g p t) o -> p g (t o)", p=P, t=4))
 
         def copy(eng, out, in_):
             if eng is S:
@@ -104,76 +97,97 @@ def tile_crystal_slip_rates_s8_kernel(
             else:
                 V.tensor_copy(out=out, in_=in_)
 
-        grp = {}
-
-        def new_grp(key):
-            grp[key] = work.tile([P, B, 4], BF16, name="grp", tag="grp", bufs=4, align_bytes=64)
-
         def bank(tag, shape):
-            return psum.tile(shape, F32, name=tag, tag=tag, bufs={"tau": 4, "out": 3, "tr": 1}[tag])
+            return psum.tile(shape, F32, name="ps" + tag, tag="ps" + tag, bufs=BANKS[tag])
 
-        def turn(key, src, wbase, t0, eng, tag="tr", off=0, step=2):
+        def spin(src, tag):
+            d = bank(tag, [P, B])
+            PE.matmul(out=d[:], lhsT=src[:, 0:P], rhs=src, start=True, stop=True)
+
+        def SPZ(tag):
+            spin(zb[:], tag)
+
+        def SPW(g, nb, t, tag):
+            spin(wide[(g, nb)][:, t, :], tag)
+
+        def SPI(g, nb, tag):
+            spin(grp[("sch", g, nb)][:, 0:P, :].rearrange("p c t -> p (c t)"), tag)
+
+        def SPS(u, t, tag):
+            spin(slip[u][:, t, :], tag)
+
+        grp, trs = {}, {}
+
+        def turn_pe(key, src, wbase, step, tag):
             tr = bank(tag, [P, 2, 2, P])
             for a in range(2):
-                words = src[:, t0 + a, :].bitcast(F32)
+                words = src[:, a, :].bitcast(F32)
                 for u in range(2):
                     w = words[:, wbase + u : wbase + 256 : 2] if step == 2 else words[:, u * P : (u + 1) * P]
                     PE.transpose(tr[:, a, u, :], w, ident[:])
-            dst = grp[key][:, (t0 - off) * P : (t0 - off + 2) * P, :].bitcast(F32)
+            trs[key] = tr
+
+        def turn_copy(key, eng):
+            grp[key] = work.tile([P, 2 * P, 4], BF16, name="half", tag="half", bufs=6, align_bytes=64)
             copy(
                 eng,
-                dst.rearrange("p (a r) u -> p a r u", a=2),
-                tr[:].rearrange("p a u r -> p a r u"),
+                grp[key][:].bitcast(F32).rearrange("p (a r) u -> p a r u", a=2),
+                trs[key][:].rearrange("p a u r -> p a r u"),
             )
 
-        def quant(key, codes, scales, c0=0, c1=B):
+        def quant(key, codes, scales, c0, c1):
             V.quantize_mx(
                 out=codes.bitcast(FP8X4),
                 scales=scales,
                 in_=grp[key][:, c0:c1, :].rearrange("p c t -> p (c t)"),
             )
 
-        def sig_turn(h, g, t0, eng, tag="tr"):
-            key = ("sig", h, g)
-            if t0 == 0:
-                new_grp(key)
-            turn(key, raw["s%d" % h], 256 * g, t0, eng, tag)
+        def ST(h, g, t0, tag):
+            turn_pe(("s", h, g, t0), raw[("s", h, t0)], 256 * g, 2, tag)
 
-        def sig_quant(h, g):
-            quant(("sig", h, g), sig_codes[:, h, g, :], sig_sc[:, h, g, :])
+        def SC(h, g, t0, eng):
+            turn_copy(("s", h, g, t0), eng)
 
-        def mem_turn(g, t0, eng, tag="tr"):
-            key = ("mem", g)
-            if t0 == 0:
-                new_grp(key)
-            turn(key, raw["m"], 256 * g, t0, eng, tag)
+        def SQ(h, g, t0):
+            c = slice(t0 * P, (t0 + 2) * P)
+            quant(("s", h, g, t0), sig_codes[:, h, g, c], sig_sc[:, h, g, c], 0, 2 * P)
 
-        def mem_quant(g):
-            quant(("mem", g), mem_codes[:, g, :], mem_sc[:, g, :])
+        def MT(g, t0, tag):
+            turn_pe(("m", g, t0), raw[("m", t0)], 256 * g, 2, tag)
+
+        def MC(g, t0, eng):
+            turn_copy(("m", g, t0), eng)
+
+        def MQ(g, t0):
+            c = slice(t0 * P, (t0 + 2) * P)
+            quant(("m", g, t0), mem_codes[:, g, c], mem_sc[:, g, c], 0, 2 * P)
 
         wide = {}
 
-        def widen(g, nb, ts, eng):
+        def W(g, nb, t, eng):
             key = (g, nb)
             if key not in wide:
                 wide[key] = work.tile([P, 4, B], BF16, name="wide", tag="wide", bufs=3, align_bytes=64)
-            for t in ts:
-                b = byt0[:, g, t, :] if nb == 0 else byt1[:, g, t, (nb - 1) * B : nb * B]
-                b = b.bitcast(FP8)
-                s = scl[:, g, t : t + 1]
-                if eng is S:
-                    S.activation(out=wide[key][:, t, :], in_=b, func=COPY, scale=s)
-                else:
-                    V.tensor_scalar(out=wide[key][:, t, :], in0=b, scalar1=s, scalar2=None, op0=MULT)
+            b = byt0[:, g, t, :] if nb == 0 else byt1[:, g, t, (nb - 1) * B : nb * B]
+            b = b.bitcast(FP8)
+            s = scl[:, g, t : t + 1]
+            if eng is S:
+                S.activation(out=wide[key][:, t, :], in_=b, func=COPY, scale=s)
+            else:
+                V.tensor_scalar(out=wide[key][:, t, :], in0=b, scalar1=s, scalar2=None, op0=MULT)
 
-        def sch_inter(g, nb, eng):
+        def new_grp(key):
+            if key not in grp:
+                grp[key] = work.tile([P, B, 4], BF16, name="grp", tag="grp", bufs=4, align_bytes=64)
+
+        def I(g, nb, eng):
             key = ("sch", g, nb)
             new_grp(key)
             copy(eng, grp[key][:], wide[(g, nb)][:].rearrange("p t n -> p n t"))
 
-        def sch_quant(g, nb):
+        def Q(g, nb):
             c = slice(nb * B, nb * B + B)
-            quant(("sch", g, nb), sch_codes[:, g, c], sch_sc[:, g, c])
+            quant(("sch", g, nb), sch_codes[:, g, c], sch_sc[:, g, c], 0, B)
 
         tau, w_sb, a_sb, slip = {}, {}, {}, {}
 
@@ -188,74 +202,78 @@ def tile_crystal_slip_rates_s8_kernel(
                 stop=stop,
             )
 
-        def do_tau(i, t):
-            h, nb = units[i]
-            ps = psum.tile([P, B], F32, name="tau", tag="tau", bufs=4)
-            c, n = slice(t * P, t * P + P), slice(nb * B, nb * B + B)
+        units = [(0, 0), (0, 1), (0, 2), (1, 0), (1, 1), (1, 2)]
+
+        def TA(u, t, tag):
+            h, nb = units[u]
+            ps = bank(tag, [P, B])
+            c, n = slice(t * P, (t + 1) * P), slice(nb * B, nb * B + B)
             for g in range(2):
                 mm(ps[:], sig_codes[:, h, g, c], sig_sc[:, h, g, c], sch_codes[:, g, n], sch_sc[:, g, n], g == 0, g == 1)
-            tau[(i, t)] = ps
+            tau[(u, t)] = ps
 
-        def half(d, i, t, name, dt, bufs):
-            key = (i, t // 2)
-            if key not in d:
-                d[key] = work.tile([P, 2, B], dt, name=name, tag=name, bufs=bufs)
-            return d[key]
+        def AB(u, t):
+            k = (u, t // 2)
+            if k not in a_sb:
+                a_sb[k] = work.tile([P, 2, B], F32, name="a_sb", tag="a_sb", bufs=3)
+            S.activation(out=a_sb[k][:, t % 2, :], in_=tau[(u, t)][:], func=ABS)
 
-        def ab(i, t):
-            a = half(a_sb, i, t, "a_sb", F32, 3)
-            S.activation(out=a[:, t % 2, :], in_=tau[(i, t)][:], func=ABS)
-
-        def v1(i, t):
-            h, nb = units[i]
-            w = half(w_sb, i, t, "w_sb", F32, 3)
+        def V1(u, t):
+            k = (u, t // 2)
+            h, nb = units[u]
+            if k not in w_sb:
+                w_sb[k] = work.tile([P, 2, B], F32, name="w_sb", tag="w_sb", bufs=2)
             V.tensor_tensor(
-                out=w[:, t % 2, :], in0=tau[(i, t)][:], in1=rate_sb[:, h, t, nb * B : nb * B + B], op=MULT
+                out=w_sb[k][:, t % 2, :],
+                in0=tau[(u, t)][:],
+                in1=rate_sb[:, h, t, nb * B : nb * B + B],
+                op=MULT,
             )
 
-        def prod(i, t0):
-            if i not in slip:
-                slip[i] = work.tile([P, 4, B], BF16, name="slip", tag="slip", bufs=4, align_bytes=64)
-            for t in (t0, t0 + 1):
-                V.tensor_tensor(
-                    out=slip[i][:, t, :].rearrange("p (u i e) -> p u i e", u=2, e=2),
-                    in0=w_sb[(i, t0 // 2)][:, t % 2, :].rearrange("p (i u e) -> p u i e", u=2, e=2),
-                    in1=a_sb[(i, t0 // 2)][:, t % 2, :].rearrange("p (i u e) -> p u i e", u=2, e=2),
-                    op=MULT,
-                )
+        def PR(u, t):
+            k = (u, t // 2)
+            if u not in slip:
+                slip[u] = work.tile([P, 4, B], BF16, name="slip", tag="slip", bufs=6, align_bytes=64)
+            V.tensor_tensor(
+                out=slip[u][:, t, :].rearrange("p (u i e) -> p u i e", u=2, e=2),
+                in0=w_sb[k][:, t % 2, :].rearrange("p (i u e) -> p u i e", u=2, e=2),
+                in1=a_sb[k][:, t % 2, :].rearrange("p (i u e) -> p u i e", u=2, e=2),
+                op=MULT,
+            )
 
-        def slip_turn(i, t0, eng, tag="tr"):
-            key = ("col", i, t0)
-            grp[key] = work.tile([P, 2 * P, 4], BF16, name="colgrp", tag="colgrp", bufs=4, align_bytes=64)
-            turn(key, slip[i], 0, t0, eng, tag, t0, 1)
+        def CT(u, t0, tag):
+            turn_pe(("c", u, t0), slip[u][:, t0 : t0 + 2, :], 0, 1, tag)
 
-        def col_quant(i, t0):
-            h, nb = units[i]
+        def CC(u, t0, eng):
+            turn_copy(("c", u, t0), eng)
+
+        def CQ(u, t0):
+            h, nb = units[u]
             c = slice(t0 * P, (t0 + 2) * P)
-            quant(("col", i, t0), col_codes[:, h, nb, c], col_sc[:, h, nb, c], 0, 2 * P)
+            quant(("c", u, t0), col_codes[:, h, nb, c], col_sc[:, h, nb, c], 0, 2 * P)
 
-        def row_inter(i, eng=V, c0=0, c1=B):
-            key = ("row", i)
-            if c0 == 0:
-                new_grp(key)
-            copy(eng, grp[key][:, c0:c1, :], slip[i][:, :, c0:c1].rearrange("p t n -> p n t"))
+        def RI(u, p, eng):
+            key = ("r", u)
+            new_grp(key)
+            c = slice(256 * p, 256 * (p + 1))
+            copy(eng, grp[key][:, c, :], slip[u][:, :, c].rearrange("p t n -> p n t"))
 
-        def row_quant(i, c0=0, c1=B):
-            h, nb = units[i]
+        def RQ(u, p):
+            h, nb = units[u]
+            c0, c1 = (0, B) if p == 2 else (256 * p, 256 * (p + 1))
             n = slice(nb * B + c0, nb * B + c1)
-            quant(("row", i), row_codes[:, h, n], row_sc[:, h, n], c0, c1)
+            quant(("r", u), row_codes[:, h, n], row_sc[:, h, n], c0, c1)
 
         strain_v = strain.rearrange("(h p t) c -> h p t c", p=P, t=4)
         acc_v = acc.rearrange("(p s) n -> p s n", s=4)
-        st2, osb = {}, {}
+        st2, st3, osb = {}, {}, {}
 
-        def st2_mm(h, t, c, gs, tag="out"):
+        def M2(h, t, c, part, tag=None):
             key = (h, t, c)
-            if key not in st2:
-                nbufs = {"out": 3, "tau": 4, "tr": 1}[tag]
-                st2[key] = psum.tile([P, B], F32, name=tag, tag=tag, bufs=nbufs)
+            if part == 0:
+                st2[key] = bank(tag, [P, B])
             m = slice(t * P, t * P + P)
-            for g in gs:
+            for g in (range(2) if part == 0 else (2,)):
                 mm(
                     st2[key][:],
                     col_codes[:, h, g, m],
@@ -267,209 +285,392 @@ def tile_crystal_slip_rates_s8_kernel(
                     fp4=True,
                 )
 
-        def st2_out(h, t, c, eng):
-            if c == 0:
+        def O2(h, t, c, eng):
+            if (h, t) not in osb:
                 osb[(h, t)] = work.tile([P, C], F32, name="osb", tag="osb", bufs=3)
-            o = osb[(h, t)]
-            copy(eng, o[:, c * B : (c + 1) * B], st2[(h, t, c)][:])
-            if c == 1:
-                nc.sync.dma_start(out=strain_v[h, :, t, :], in_=o[:])
+            copy(eng, osb[(h, t)][:, c * B : (c + 1) * B], st2[(h, t, c)][:])
 
-        def st2_full(h, t, c, eng, tag="out"):
-            st2_mm(h, t, c, range(3), tag)
-            st2_out(h, t, c, eng)
+        def D2(h, t):
+            nc.sync.dma_start(out=strain_v[h, :, t, :], in_=osb[(h, t)][:])
 
-        st3, oacc = {}, {}
-
-        def st3_mm(nb, s, c0=0, c1=B, tag="out"):
+        def M3(nb, s, p, tag=None):
             key = (nb, s)
-            if c0 == 0:
-                nbufs = {"out": 3, "tau": 4, "tr": 1}[tag]
-                st3[key] = psum.tile([P, B], F32, name=tag, tag=tag, bufs=nbufs)
+            if p != 1:
+                st3[key] = bank(tag, [P, B])
+            c0, c1 = (0, B) if p == 2 else (256 * p, 256 * (p + 1))
             m, n = slice(s * P, s * P + P), slice(nb * B + c0, nb * B + c1)
             for h in range(2):
                 mm(st3[key][:, c0:c1], mem_codes[:, h, m], mem_sc[:, h, m], row_codes[:, h, n], row_sc[:, h, n], h == 0, h == 1)
 
-        def st3_out(nb, s, eng):
+        oacc = {}
+
+        def O3(nb, s, eng):
             o = work.tile([P, B], F32, name="oacc", tag="oacc", bufs=5)
+            oacc[(nb, s)] = o
             copy(
                 eng,
                 o[:].rearrange("p (i u e) -> p i u e", u=2, e=2),
                 st3[(nb, s)][:].rearrange("p (u i e) -> p i u e", u=2, e=2),
             )
-            nc.sync.dma_start(out=acc_v[:, s, nb * B : nb * B + B], in_=o[:])
 
-        def st3_full(nb, s, eng, tag="out"):
-            st3_mm(nb, s, tag=tag)
-            st3_out(nb, s, eng)
+        def D3(nb, s):
+            nc.sync.dma_start(out=acc_v[:, s, nb * B : nb * B + B], in_=oacc[(nb, s)][:])
 
-        units = [(0, 0), (0, 1), (0, 2), (1, 0), (1, 1), (1, 2)]
-
-        if MANUAL:
-            ctx.enter_context(
-                tc.manual_schedule(
-                    engines={mybir.EngineType.PE, mybir.EngineType.Activation, mybir.EngineType.DVE}
-                )
-            )
-
-        widen(0, 0, (0,), S)
-        widen(0, 0, (1, 2, 3), V)
-        widen(1, 0, (0,1), S)
-        sch_inter(0, 0, V)
-        widen(1, 0, (2, 3), V)
-        sch_quant(0, 0)
-        sig_turn(0, 0, 0, S)
-        sig_turn(0, 1, 0, S, "out")
-        sch_inter(1, 0, V)
-        sig_turn(0, 0, 2, S, "out")
-        sig_turn(0, 1, 2, S, "out")
-        sch_quant(1, 0)
-        sig_quant(0, 0)
-        sig_quant(0, 1)
-
-        L = lambda f, *a: (lambda: f(*a))
-
-        def run(fs):
-            for f in fs:
-                f()
-
-        for t in range(4):
-            do_tau(0, t)
-        widen(0, 1, range(4), S)
-        for t in range(4):
-            v1(0, t)
-            ab(0, t)
-
-        prod(0, 0)
-        slip_turn(0, 0, S)
-        prod(0, 2)
-        widen(1, 1, range(2), S)
-        slip_turn(0, 2, S, "out")
-        sch_inter(0, 1, V)
-        widen(1, 1, range(2, 4), S)
-        row_inter(0)
-        sch_quant(0, 1)
-        sch_inter(1, 1, V)
-        widen(0, 2, range(4), S)
-        col_quant(0, 0)
-        col_quant(0, 2)
-        sch_quant(1, 1)
-        for t in range(4):
-            do_tau(1, t)
-        row_quant(0)
-        sch_inter(0, 2, S)
-        for t in range(4):
-            v1(1, t)
-            ab(1, t)
-        widen(1, 2, range(4), S)
-        sch_quant(0, 2)
-        prod(1, 0)
-        slip_turn(1, 0, S)
-        prod(1, 2)
-        slip_turn(1, 2, S, "out")
-        row_inter(1)
-        sch_inter(1, 2, V)
-        sig_turn(1, 0, 0, S)
-        sig_turn(1, 1, 0, S, "out")
-        sig_turn(1, 0, 2, S, "out")
-        sig_turn(1, 1, 2, S, "out")
-        col_quant(1, 0)
-        col_quant(1, 2)
-        sch_quant(1, 2)
-        mem_fill = [L(mem_turn, 0, 0, S), L(mem_turn, 1, 0, S, "out"), L(mem_turn, 0, 2, S, "out"), L(mem_turn, 1, 2, S, "out")]
-        run(mem_fill[:2])
-        for t in range(4):
-            do_tau(2, t)
-        row_quant(1)
-        sig_quant(1, 0)
-        v1(2, 0)
-        v1(2, 1)
-        ab(2, 0)
-        ab(2, 1)
-        sig_quant(1, 1)
-
-        st2a = [L(st2_full, 0, t, c, S) for t in range(2) for c in range(2)]
-        st2b = [L(st2_full, 0, t, c, S) for t in range(2, 4) for c in range(2)]
-        st2c = [L(st2_full, 1, t, c, S) for t in range(2) for c in range(2)]
-        st3a = [L(st3_full, 0, s, S) for s in range(4)]
-        st3b = [L(st3_full, 1, s, S) for s in range(4)]
-
-        halves = [(2, 0), (2, 2), (3, 0), (4, 0), (5, 0), (3, 2), (4, 2), (5, 2)]
-
-        def front(k):
-            i, t0 = halves[k]
-            for t in (t0, t0 + 1):
-                v1(i, t)
-                if k + 2 < len(halves):
-                    do_tau(halves[k + 2][0], halves[k + 2][1] + t - t0)
-
-        def absk(k):
-            if k < len(halves):
-                i, t0 = halves[k]
-                ab(i, t0)
-                ab(i, t0 + 1)
-
-        def back(k, fill):
-            i, t0 = halves[k]
-            prod(i, t0)
-            absk(k + 1)
-            slip_turn(i, t0, S)
-            run(fill)
-
-        def cq(k):
-            col_quant(*halves[k])
-
-        do_tau(3, 0)
-        do_tau(3, 1)
-        back(0, mem_fill[2:])
-        front(1)
-        cq(0)
-        back(1, st2a)
-        row_inter(2)
-        mem_quant(0)
-        front(2)
-        cq(1)
-        row_quant(2)
-        back(2, st2b[:2])
-        front(3)
-        cq(2)
-        back(3, st2b[2:])
-        mem_quant(1)
-        front(4)
-        cq(3)
-        back(4, [])
-        front(5)
-        cq(4)
-        back(5, st2c)
-        row_inter(3)
-        front(6)
-        cq(5)
-        row_quant(3)
-        back(6, st3a)
-        row_inter(4)
-        front(7)
-        cq(6)
-        row_quant(4)
-        for t in range(2, 4):
-            for c in range(2):
-                st2_mm(1, t, c, range(2), "tau")
-        prod(5, 2)
-        slip_turn(5, 2, S)
-        row_inter(5, V, 0, 256)
-        run(st3b)
-        col_quant(5, 2)
-        row_quant(5, 0, 256)
-        row_inter(5, V, 256, 512)
-        for t in range(2, 4):
-            for c in range(2):
-                st2_mm(1, t, c, (2,), "tau")
-        for t in range(2, 4):
-            for c in range(2):
-                st2_out(1, t, c, (S, V)[c])
-        for s in range(4):
-            st3_mm(2, s, 0, 256, ("out", "out", "out", "tr")[s])
-        row_quant(5, 256, 512)
-        for s in range(4):
-            st3_mm(2, s, 256, 512)
-        for s in range(4):
-            st3_out(2, s, (S, V)[s % 2])
+        ctx.enter_context(
+            tc.manual_schedule(engines={mybir.EngineType.PE, mybir.EngineType.Activation, mybir.EngineType.DVE, mybir.EngineType.SP})
+        )
+        load_scale()
+        load_bytes(0, 0)
+        W(0, 0, 1, V)
+        W(0, 0, 3, V)
+        SPW(0, 0, 3, "A")
+        W(0, 0, 0, V)
+        load_bytes(1, 0)
+        W(1, 0, 0, V)
+        W(0, 0, 2, S)
+        I(0, 0, V)
+        load_bytes(0, 1)
+        SPW(0, 0, 3, "A")
+        W(0, 1, 2, V)
+        SPZ("C")
+        W(1, 0, 3, S)
+        W(1, 0, 1, S)
+        load_sigma(1, 0)
+        SPW(1, 0, 3, "C")
+        W(1, 0, 2, S)
+        W(0, 2, 3, V)
+        W(0, 1, 1, S)
+        load_sigma(0, 0)
+        I(1, 0, V)
+        SPW(1, 0, 3, "C")
+        W(0, 1, 3, S)
+        W(0, 1, 0, S)
+        Q(0, 0)
+        I(0, 1, V)
+        W(0, 2, 0, S)
+        ST(1, 1, 0, "B")
+        SC(1, 1, 0, S)
+        load_bytes(1, 1)
+        W(1, 1, 0, V)
+        W(0, 2, 1, S)
+        ST(1, 0, 0, "A")
+        Q(1, 0)
+        ST(0, 0, 0, "A")
+        SC(0, 0, 0, S)
+        SPI(1, 0, "A")
+        SQ(0, 0, 0)
+        W(0, 2, 2, V)
+        W(1, 1, 3, V)
+        SPI(1, 0, "A")
+        W(1, 1, 2, V)
+        ST(0, 1, 0, "B")
+        SC(0, 1, 0, S)
+        SQ(0, 1, 0)
+        SC(1, 0, 0, S)
+        W(1, 1, 1, S)
+        SQ(1, 0, 0)
+        I(1, 1, V)
+        I(0, 2, S)
+        SPZ("B")
+        TA(0, 0, "B")
+        W(1, 2, 3, V)
+        load_sigma(0, 2)
+        ST(0, 1, 2, "B")
+        Q(0, 1)
+        load_rate(0, 0, 512)
+        SC(0, 1, 2, S)
+        Q(1, 1)
+        W(1, 2, 2, V)
+        W(1, 2, 0, S)
+        SPZ("A")
+        TA(0, 1, "A")
+        V1(0, 1)
+        SPZ("A")
+        TA(1, 1, "B")
+        load_rate(0, 512, 1536)
+        V1(1, 1)
+        AB(0, 0)
+        Q(0, 2)
+        AB(0, 1)
+        TA(1, 0, "A")
+        AB(1, 0)
+        V1(0, 0)
+        W(1, 2, 1, S)
+        load_rows(("m", 2), mem, 2)
+        SQ(1, 1, 0)
+        ST(0, 0, 2, "A")
+        AB(1, 1)
+        SC(0, 0, 2, S)
+        SPZ("C")
+        I(1, 2, S)
+        TA(3, 0, "A")
+        AB(3, 0)
+        V1(1, 0)
+        SPI(1, 1, "C")
+        PR(0, 0)
+        SPZ("B")
+        PR(1, 0)
+        SPZ("C")
+        SQ(0, 0, 2)
+        load_rows(("m", 0), mem, 0)
+        TA(4, 1, "A")
+        PR(0, 1)
+        AB(4, 1)
+        MT(0, 0, "B")
+        load_rate(1, 0, 1536)
+        load_sigma(1, 2)
+        PR(1, 1)
+        SQ(0, 1, 2)
+        MC(0, 0, S)
+        TA(3, 1, "B")
+        SPI(1, 1, "C")
+        V1(3, 1)
+        Q(1, 2)
+        V1(3, 0)
+        V1(4, 1)
+        SPS(0, 1, "A")
+        TA(4, 0, "A")
+        MT(1, 0, "C")
+        MC(1, 0, S)
+        V1(4, 0)
+        CT(0, 0, "B")
+        MQ(0, 0)
+        TA(2, 0, "A")
+        MQ(1, 0)
+        SPS(0, 1, "A")
+        AB(3, 1)
+        AB(4, 0)
+        TA(2, 1, "A")
+        AB(2, 1)
+        ST(1, 0, 2, "B")
+        PR(3, 0)
+        AB(2, 0)
+        PR(3, 1)
+        CC(0, 0, S)
+        SPS(1, 1, "C")
+        V1(2, 1)
+        load_back()
+        PR(4, 0)
+        SC(1, 0, 2, S)
+        TA(0, 2, "B")
+        AB(0, 2)
+        TA(0, 3, "A")
+        AB(0, 3)
+        V1(2, 0)
+        CT(3, 0, "C")
+        PR(4, 1)
+        TA(1, 2, "B")
+        CC(3, 0, S)
+        PR(2, 1)
+        AB(1, 2)
+        ST(1, 1, 2, "A")
+        PR(2, 0)
+        CT(4, 0, "A")
+        CC(4, 0, S)
+        CT(1, 0, "C")
+        CC(1, 0, S)
+        CQ(0, 0)
+        CT(2, 0, "A")
+        TA(5, 0, "B")
+        SC(1, 1, 2, S)
+        AB(5, 0)
+        SQ(1, 0, 2)
+        TA(5, 1, "C")
+        CC(2, 0, S)
+        AB(5, 1)
+        V1(0, 2)
+        V1(0, 3)
+        V1(1, 2)
+        PR(0, 2)
+        TA(1, 3, "A")
+        AB(1, 3)
+        SPS(1, 1, "A")
+        MT(0, 2, "B")
+        MC(0, 2, S)
+        PR(0, 3)
+        RI(0, 0, S)
+        CQ(1, 0)
+        M2(0, 1, 1, 0, "A")
+        CQ(2, 0)
+        M2(0, 1, 0, 0, "A")
+        V1(5, 1)
+        M2(0, 1, 1, 1)
+        M2(0, 1, 0, 1)
+        TA(2, 2, "C")
+        O2(0, 1, 1, S)
+        V1(1, 3)
+        M2(0, 0, 1, 0, "B")
+        M2(0, 0, 1, 1)
+        V1(5, 0)
+        PR(1, 2)
+        AB(2, 2)
+        TA(2, 3, "A")
+        CQ(4, 0)
+        MQ(0, 2)
+        M2(0, 0, 0, 0, "B")
+        PR(1, 3)
+        SQ(1, 1, 2)
+        TA(3, 3, "A")
+        V1(2, 2)
+        CT(1, 2, "B")
+        O2(0, 1, 0, S)
+        AB(2, 3)
+        D2(0, 1)
+        O2(0, 0, 1, S)
+        PR(5, 1)
+        PR(5, 0)
+        AB(3, 3)
+        M2(0, 0, 0, 1)
+        O2(0, 0, 0, S)
+        V1(2, 3)
+        CQ(3, 0)
+        V1(3, 3)
+        TA(4, 2, "B")
+        AB(4, 2)
+        TA(3, 2, "A")
+        PR(2, 3)
+        CT(0, 2, "A")
+        AB(3, 2)
+        CC(0, 2, S)
+        CC(1, 2, S)
+        CT(5, 0, "B")
+        MT(1, 2, "C")
+        TA(5, 2, "A")
+        CC(5, 0, S)
+        PR(2, 2)
+        CT(2, 2, "B")
+        V1(4, 2)
+        MC(1, 2, V)
+        AB(5, 2)
+        PR(3, 3)
+        D2(0, 0)
+        M2(1, 0, 0, 0, "B")
+        MQ(1, 2)
+        CQ(5, 0)
+        M2(1, 0, 0, 1)
+        RI(1, 1, S)
+        M2(1, 0, 1, 0, "C")
+        V1(3, 2)
+        CQ(0, 2)
+        CC(2, 2, S)
+        O2(1, 0, 0, S)
+        M2(1, 0, 1, 1)
+        PR(3, 2)
+        V1(5, 2)
+        O2(1, 0, 1, S)
+        TA(5, 3, "B")
+        RI(3, 0, S)
+        CQ(2, 2)
+        D2(1, 0)
+        TA(4, 3, "A")
+        AB(4, 3)
+        SPZ("C")
+        M2(1, 1, 1, 0, "A")
+        PR(4, 2)
+        M2(1, 1, 1, 1)
+        RI(1, 0, S)
+        CQ(1, 2)
+        V1(5, 3)
+        M2(0, 3, 1, 0, "C")
+        M2(0, 3, 1, 1)
+        O2(0, 3, 1, S)
+        O2(1, 1, 1, S)
+        RI(3, 1, V)
+        RI(0, 1, V)
+        RQ(3, 2)
+        RQ(0, 2)
+        M2(1, 1, 0, 0, "B")
+        V1(4, 3)
+        PR(5, 2)
+        AB(5, 3)
+        PR(5, 3)
+        M2(1, 1, 0, 1)
+        O2(1, 1, 0, S)
+        D2(1, 1)
+        M2(0, 3, 0, 0, "A")
+        M2(0, 3, 0, 1)
+        O2(0, 3, 0, S)
+        CT(3, 2, "C")
+        CC(3, 2, S)
+        M3(0, 3, 2, "B")
+        O3(0, 3, V)
+        D2(0, 3)
+        M3(0, 2, 2, "B")
+        O3(0, 2, S)
+        PR(4, 3)
+        RQ(1, 2)
+        D3(0, 3)
+        M2(0, 2, 0, 0, "B")
+        M2(0, 2, 0, 1)
+        O2(0, 2, 0, S)
+        RI(4, 0, S)
+        CT(5, 2, "A")
+        M2(0, 2, 1, 0, "A")
+        M2(0, 2, 1, 1)
+        RI(4, 1, V)
+        O2(0, 2, 1, V)
+        D3(0, 2)
+        M3(0, 0, 2, "A")
+        O3(0, 0, V)
+        RQ(4, 2)
+        D2(0, 2)
+        CC(5, 2, V)
+        CQ(3, 2)
+        CT(4, 2, "C")
+        CC(4, 2, S)
+        CQ(5, 2)
+        RI(5, 1, S)
+        M3(0, 1, 2, "B")
+        D3(0, 0)
+        M3(1, 0, 2, "A")
+        O3(1, 0, S)
+        D3(1, 0)
+        M3(1, 3, 2, "B")
+        M3(1, 2, 2, "A")
+        CQ(4, 2)
+        M2(1, 2, 1, 0, "A")
+        RI(5, 0, V)
+        O3(1, 3, S)
+        D3(1, 3)
+        O3(0, 1, S)
+        D3(0, 1)
+        O3(1, 2, S)
+        D3(1, 2)
+        RI(2, 1, V)
+        M2(1, 2, 0, 0, "A")
+        RI(2, 0, V)
+        M2(1, 2, 0, 1)
+        O2(1, 2, 0, S)
+        M2(1, 2, 1, 1)
+        RQ(5, 0)
+        O2(1, 2, 1, S)
+        D2(1, 2)
+        M3(1, 1, 2, "C")
+        RQ(2, 2)
+        M2(1, 3, 0, 0, "B")
+        M2(1, 3, 0, 1)
+        RQ(5, 1)
+        O3(1, 1, S)
+        D3(1, 1)
+        M3(2, 1, 0, "A")
+        O2(1, 3, 0, S)
+        M3(2, 1, 1)
+        O3(2, 1, V)
+        M3(2, 2, 0, "B")
+        M3(2, 2, 1)
+        D3(2, 1)
+        O3(2, 2, V)
+        D3(2, 2)
+        M2(1, 3, 1, 0, "C")
+        M2(1, 3, 1, 1)
+        O2(1, 3, 1, S)
+        D2(1, 3)
+        M3(2, 0, 0, "A")
+        M3(2, 0, 1)
+        O3(2, 0, V)
+        D3(2, 0)
+        SPZ("B")
+        M3(2, 3, 0, "C")
+        M3(2, 3, 1)
+        O3(2, 3, V)
+        D3(2, 3)

@@ -12,6 +12,7 @@ FP8 = mybir.dt.float8_e4m3fn
 FP8X4 = mybir.dt.float8_e4m3fn_x4
 FP4X4 = mybir.dt.float4_e2m1fn_x4
 MULT = mybir.AluOpType.mult
+ADD = mybir.AluOpType.add
 ABS = mybir.ActivationFunctionType.Abs
 COPY = mybir.ActivationFunctionType.Copy
 
@@ -26,7 +27,7 @@ def tile_crystal_slip_rates_s8_kernel(
     tc, sigma, schmid_bytes, schmid_scale, rate, back_words, back_scales, mem, strain, acc
 ):
     nc = tc.nc
-    S, V, PE = nc.scalar, nc.vector, nc.tensor
+    S, V, PE, G = nc.scalar, nc.vector, nc.tensor, nc.gpsimd
     with ExitStack() as ctx:
         keep = ctx.enter_context(tc.tile_pool(name="keep", bufs=1))
         work = ctx.enter_context(tc.tile_pool(name="work", bufs=2))
@@ -36,8 +37,7 @@ def tile_crystal_slip_rates_s8_kernel(
         touch = keep.tile([P, 8], F32, name="touch")
         zb = keep.tile([P, B], BF16, name="zb")
         scl = keep.tile([P, 2, 4], F32, name="scl")
-        byt0 = keep.tile([P, 2, 4, B], U8, name="byt0")
-        byt1 = keep.tile([P, 2, 4, 2 * B], U8, name="byt1")
+        byt = keep.tile([P, 2, 4, N], U8, name="byt")
         rate_sb = keep.tile([P, 2, 4, N], BF16, name="rate_sb")
         sig_codes = keep.tile([P, 2, 2, B], U32, name="sig_codes", align_bytes=64)
         sig_sc = keep.tile([P, 2, 2, B], U8, name="sig_sc", align_bytes=64)
@@ -68,17 +68,13 @@ def tile_crystal_slip_rates_s8_kernel(
         def load_sigma(h, t0):
             load_rows(("s", h, t0), sigma[h * B : (h + 1) * B, :], t0)
 
-        def load_bytes(g, rest):
+        def load_bytes(g, t0):
             v = schmid_bytes[g * B : (g + 1) * B, :].rearrange("(p t) n -> p t n", t=4)
-            if rest:
-                nc.sync.dma_start(out=byt1[:, g], in_=v[:, :, B:])
-            else:
-                nc.sync.dma_start(out=byt0[:, g], in_=v[:, :, 0:B])
+            nc.sync.dma_start(out=byt[:, g, t0 : t0 + 2], in_=v[:, t0 : t0 + 2, :])
 
-        def load_rate(h, n0, n1):
-            nc.sync.dma_start(
-                out=rate_sb[:, h, :, n0:n1], in_=rate[h * B : (h + 1) * B, n0:n1].rearrange("(p t) n -> p t n", t=4)
-            )
+        def load_rate(h, t0):
+            v = rate[h * B : (h + 1) * B, :].rearrange("(p t) n -> p t n", t=4)
+            nc.sync.dma_start(out=rate_sb[:, h, t0 : t0 + 2], in_=v[:, t0 : t0 + 2, :])
 
         def load_back():
             nc.sync.dma_start(out=bw[:].bitcast(I32), in_=back_words.rearrange("g p w -> p g w").bitcast(I32))
@@ -89,13 +85,18 @@ def tile_crystal_slip_rates_s8_kernel(
                 )
 
         def load_scale():
-            nc.sync.dma_start(out=scl[:], in_=schmid_scale.rearrange("(g p t) o -> p g (t o)", p=P, t=4))
+            nc.scalar.dma_start(out=scl[:], in_=schmid_scale.rearrange("(g p t) o -> p g (t o)", p=P, t=4))
 
         def copy(eng, out, in_):
             if eng is S:
                 S.copy(out=out, in_=in_)
+            elif eng is G:
+                G.tensor_scalar(out=out, in0=in_, scalar1=1.0, scalar2=0.0, op0=MULT, op1=ADD)
             else:
                 V.tensor_copy(out=out, in_=in_)
+
+        def weave(eng, out, in_):
+            copy(eng, out.rearrange("p (c i) t -> p c t i", i=4), in_.rearrange("p t (c i) -> p c t i", i=4))
 
         def bank(tag, shape):
             return psum.tile(shape, F32, name="ps" + tag, tag="ps" + tag, bufs=BANKS[tag])
@@ -168,7 +169,7 @@ def tile_crystal_slip_rates_s8_kernel(
             key = (g, nb)
             if key not in wide:
                 wide[key] = work.tile([P, 4, B], BF16, name="wide", tag="wide", bufs=3, align_bytes=64)
-            b = byt0[:, g, t, :] if nb == 0 else byt1[:, g, t, (nb - 1) * B : nb * B]
+            b = byt[:, g, t, nb * B : (nb + 1) * B]
             b = b.bitcast(FP8)
             s = scl[:, g, t : t + 1]
             if eng is S:
@@ -183,7 +184,7 @@ def tile_crystal_slip_rates_s8_kernel(
         def I(g, nb, eng):
             key = ("sch", g, nb)
             new_grp(key)
-            copy(eng, grp[key][:], wide[(g, nb)][:].rearrange("p t n -> p n t"))
+            weave(eng, grp[key][:], wide[(g, nb)][:])
 
         def Q(g, nb):
             c = slice(nb * B, nb * B + B)
@@ -230,11 +231,11 @@ def tile_crystal_slip_rates_s8_kernel(
                 op=MULT,
             )
 
-        def PR(u, t):
+        def PR(u, t, eng):
             k = (u, t // 2)
             if u not in slip:
                 slip[u] = work.tile([P, 4, B], BF16, name="slip", tag="slip", bufs=6, align_bytes=64)
-            V.tensor_tensor(
+            eng.tensor_tensor(
                 out=slip[u][:, t, :].rearrange("p (u i e) -> p u i e", u=2, e=2),
                 in0=w_sb[k][:, t % 2, :].rearrange("p (i u e) -> p u i e", u=2, e=2),
                 in1=a_sb[k][:, t % 2, :].rearrange("p (i u e) -> p u i e", u=2, e=2),
@@ -256,7 +257,7 @@ def tile_crystal_slip_rates_s8_kernel(
             key = ("r", u)
             new_grp(key)
             c = slice(256 * p, 256 * (p + 1))
-            copy(eng, grp[key][:, c, :], slip[u][:, :, c].rearrange("p t n -> p n t"))
+            weave(eng, grp[key][:, c, :], slip[u][:, :, c])
 
         def RQ(u, p):
             h, nb = units[u]
@@ -317,360 +318,361 @@ def tile_crystal_slip_rates_s8_kernel(
             nc.sync.dma_start(out=acc_v[:, s, nb * B : nb * B + B], in_=oacc[(nb, s)][:])
 
         ctx.enter_context(
-            tc.manual_schedule(engines={mybir.EngineType.PE, mybir.EngineType.Activation, mybir.EngineType.DVE, mybir.EngineType.SP})
+            tc.manual_schedule(engines={mybir.EngineType.PE, mybir.EngineType.Activation, mybir.EngineType.DVE, mybir.EngineType.SP, mybir.EngineType.Pool})
         )
         load_scale()
+        SPZ("A")
+        load_bytes(0, 2)
+        W(0, 0, 2, V)
+        W(0, 2, 3, V)
+        W(0, 0, 3, V)
+        SPW(0, 0, 3, "B")
+        W(0, 2, 2, V)
+        W(0, 1, 3, S)
+        W(0, 1, 2, S)
+        SPZ("B")
         load_bytes(0, 0)
         W(0, 0, 1, V)
-        W(0, 0, 3, V)
-        SPW(0, 0, 3, "A")
-        W(0, 0, 0, V)
-        load_bytes(1, 0)
-        W(1, 0, 0, V)
-        W(0, 0, 2, S)
-        I(0, 0, V)
-        load_bytes(0, 1)
-        SPW(0, 0, 3, "A")
-        W(0, 1, 2, V)
-        SPZ("C")
-        W(1, 0, 3, S)
-        W(1, 0, 1, S)
-        load_sigma(1, 0)
-        SPW(1, 0, 3, "C")
-        W(1, 0, 2, S)
-        W(0, 2, 3, V)
-        W(0, 1, 1, S)
-        load_sigma(0, 0)
-        I(1, 0, V)
-        SPW(1, 0, 3, "C")
-        W(0, 1, 3, S)
         W(0, 1, 0, S)
-        Q(0, 0)
-        I(0, 1, V)
-        W(0, 2, 0, S)
-        ST(1, 1, 0, "B")
-        SC(1, 1, 0, S)
-        load_bytes(1, 1)
-        W(1, 1, 0, V)
+        W(0, 0, 0, V)
+        W(0, 2, 0, V)
+        I(0, 0, V)
+        W(0, 1, 1, S)
+        SPZ("B")
+        load_bytes(1, 0)
         W(0, 2, 1, S)
-        ST(1, 0, 0, "A")
-        Q(1, 0)
+        SPZ("A")
+        I(0, 2, V)
+        Q(0, 0)
+        SPW(0, 0, 3, "A")
+        I(0, 1, S)
+        W(1, 0, 1, S)
+        SPZ("B")
+        load_sigma(0, 0)
+        ST(0, 1, 0, "A")
+        SPZ("B")
         ST(0, 0, 0, "A")
-        SC(0, 0, 0, S)
-        SPI(1, 0, "A")
-        SQ(0, 0, 0)
-        W(0, 2, 2, V)
-        W(1, 1, 3, V)
-        SPI(1, 0, "A")
-        W(1, 1, 2, V)
-        ST(0, 1, 0, "B")
-        SC(0, 1, 0, S)
-        SQ(0, 1, 0)
-        SC(1, 0, 0, S)
-        W(1, 1, 1, S)
-        SQ(1, 0, 0)
-        I(1, 1, V)
-        I(0, 2, S)
-        SPZ("B")
-        TA(0, 0, "B")
-        W(1, 2, 3, V)
-        load_sigma(0, 2)
-        ST(0, 1, 2, "B")
-        Q(0, 1)
-        load_rate(0, 0, 512)
-        SC(0, 1, 2, S)
-        Q(1, 1)
-        W(1, 2, 2, V)
-        W(1, 2, 0, S)
-        SPZ("A")
-        TA(0, 1, "A")
-        V1(0, 1)
-        SPZ("A")
-        TA(1, 1, "B")
-        load_rate(0, 512, 1536)
-        V1(1, 1)
-        AB(0, 0)
+        load_bytes(1, 2)
+        W(1, 1, 2, S)
         Q(0, 2)
-        AB(0, 1)
-        TA(1, 0, "A")
-        AB(1, 0)
-        V1(0, 0)
-        W(1, 2, 1, S)
-        load_rows(("m", 2), mem, 2)
-        SQ(1, 1, 0)
-        ST(0, 0, 2, "A")
-        AB(1, 1)
-        SC(0, 0, 2, S)
-        SPZ("C")
-        I(1, 2, S)
-        TA(3, 0, "A")
-        AB(3, 0)
-        V1(1, 0)
-        SPI(1, 1, "C")
-        PR(0, 0)
+        W(1, 2, 2, V)
+        W(1, 0, 3, V)
+        SPW(1, 0, 3, "B")
+        load_sigma(1, 0)
+        Q(0, 1)
+        SPW(1, 0, 3, "B")
+        W(1, 0, 0, V)
+        W(1, 1, 1, V)
+        ST(1, 0, 0, "A")
         SPZ("B")
-        PR(1, 0)
-        SPZ("C")
-        SQ(0, 0, 2)
-        load_rows(("m", 0), mem, 0)
-        TA(4, 1, "A")
-        PR(0, 1)
-        AB(4, 1)
-        MT(0, 0, "B")
-        load_rate(1, 0, 1536)
+        W(1, 2, 1, S)
+        W(1, 1, 0, V)
+        SC(0, 1, 0, S)
+        ST(1, 1, 0, "C")
+        W(1, 1, 3, V)
         load_sigma(1, 2)
-        PR(1, 1)
-        SQ(0, 1, 2)
-        MC(0, 0, S)
-        TA(3, 1, "B")
-        SPI(1, 1, "C")
-        V1(3, 1)
-        Q(1, 2)
-        V1(3, 0)
-        V1(4, 1)
-        SPS(0, 1, "A")
-        TA(4, 0, "A")
-        MT(1, 0, "C")
-        MC(1, 0, S)
-        V1(4, 0)
-        CT(0, 0, "B")
-        MQ(0, 0)
-        TA(2, 0, "A")
-        MQ(1, 0)
-        SPS(0, 1, "A")
-        AB(3, 1)
-        AB(4, 0)
-        TA(2, 1, "A")
-        AB(2, 1)
         ST(1, 0, 2, "B")
-        PR(3, 0)
-        AB(2, 0)
-        PR(3, 1)
-        CC(0, 0, S)
-        SPS(1, 1, "C")
-        V1(2, 1)
-        load_back()
-        PR(4, 0)
+        SQ(0, 1, 0)
+        I(1, 1, V)
+        SPI(1, 1, "A")
+        W(1, 0, 2, S)
+        I(1, 0, V)
+        W(1, 2, 3, S)
+        SC(0, 0, 0, S)
+        SQ(0, 0, 0)
+        SC(1, 0, 0, S)
+        SC(1, 1, 0, S)
+        W(1, 2, 0, S)
+        Q(1, 0)
+        TA(0, 0, "A")
+        Q(1, 1)
+        TA(1, 1, "C")
+        SQ(1, 0, 0)
+        load_rate(0, 0)
+        V1(0, 0)
+        V1(1, 1)
+        TA(0, 1, "B")
+        V1(0, 1)
+        SPI(1, 0, "A")
+        SQ(1, 1, 0)
+        TA(1, 0, "A")
         SC(1, 0, 2, S)
-        TA(0, 2, "B")
-        AB(0, 2)
-        TA(0, 3, "A")
-        AB(0, 3)
-        V1(2, 0)
-        CT(3, 0, "C")
-        PR(4, 1)
-        TA(1, 2, "B")
-        CC(3, 0, S)
-        PR(2, 1)
-        AB(1, 2)
-        ST(1, 1, 2, "A")
-        PR(2, 0)
-        CT(4, 0, "A")
-        CC(4, 0, S)
-        CT(1, 0, "C")
-        CC(1, 0, S)
-        CQ(0, 0)
-        CT(2, 0, "A")
-        TA(5, 0, "B")
-        SC(1, 1, 2, S)
-        AB(5, 0)
+        I(1, 2, S)
+        V1(1, 0)
+        Q(1, 2)
+        AB(0, 0)
+        PR(0, 0, V)
+        load_sigma(0, 2)
+        AB(0, 1)
+        ST(0, 0, 2, "B")
+        PR(0, 1, V)
+        AB(1, 1)
+        AB(1, 0)
         SQ(1, 0, 2)
-        TA(5, 1, "C")
-        CC(2, 0, S)
-        AB(5, 1)
-        V1(0, 2)
-        V1(0, 3)
-        V1(1, 2)
-        PR(0, 2)
-        TA(1, 3, "A")
-        AB(1, 3)
-        SPS(1, 1, "A")
+        SC(0, 0, 2, S)
+        ST(1, 1, 2, "A")
+        PR(1, 0, V)
+        TA(2, 1, "B")
+        ST(0, 1, 2, "A")
+        PR(1, 1, V)
+        SQ(0, 0, 2)
+        load_rows(("m", 2), mem, 2)
         MT(0, 2, "B")
+        AB(2, 1)
+        V1(2, 1)
+        SC(0, 1, 2, S)
+        SQ(0, 1, 2)
         MC(0, 2, S)
-        PR(0, 3)
-        RI(0, 0, S)
+        TA(3, 1, "A")
+        AB(3, 1)
+        TA(3, 0, "C")
+        AB(3, 0)
+        TA(2, 0, "B")
+        SC(1, 1, 2, S)
+        PR(2, 1, V)
+        CT(1, 0, "A")
+        V1(2, 0)
+        load_rate(1, 0)
+        V1(3, 0)
+        MT(1, 2, "B")
+        SQ(1, 1, 2)
+        CC(1, 0, S)
+        SPI(1, 1, "B")
+        V1(3, 1)
+        AB(2, 0)
+        PR(2, 0, V)
+        PR(3, 0, V)
+        TA(4, 0, "A")
+        AB(4, 0)
+        load_rows(("m", 0), mem, 0)
+        MC(1, 2, S)
+        MQ(1, 2)
+        TA(4, 1, "C")
+        MQ(0, 2)
+        AB(4, 1)
+        PR(3, 1, V)
+        CT(0, 0, "B")
+        CC(0, 0, S)
+        MT(1, 0, "A")
+        V1(4, 0)
+        V1(4, 1)
+        TA(1, 2, "A")
+        AB(1, 2)
+        TA(1, 3, "A")
+        MC(1, 0, S)
+        CT(2, 0, "B")
+        load_rate(0, 2)
+        MT(0, 0, "B")
+        CC(2, 0, S)
+        load_back()
+        MC(0, 0, S)
         CQ(1, 0)
-        M2(0, 1, 1, 0, "A")
+        TA(0, 3, "B")
+        CQ(0, 0)
+        PR(4, 0, V)
+        TA(0, 2, "A")
         CQ(2, 0)
-        M2(0, 1, 0, 0, "A")
-        V1(5, 1)
-        M2(0, 1, 1, 1)
-        M2(0, 1, 0, 1)
-        TA(2, 2, "C")
-        O2(0, 1, 1, S)
-        V1(1, 3)
+        AB(0, 3)
+        AB(0, 2)
+        AB(1, 3)
+        PR(4, 1, V)
+        V1(1, 2)
+        V1(0, 3)
+        TA(4, 3, "A")
+        SPI(1, 0, "C")
+        AB(4, 3)
         M2(0, 0, 1, 0, "B")
         M2(0, 0, 1, 1)
-        V1(5, 0)
-        PR(1, 2)
-        AB(2, 2)
-        TA(2, 3, "A")
-        CQ(4, 0)
-        MQ(0, 2)
-        M2(0, 0, 0, 0, "B")
-        PR(1, 3)
-        SQ(1, 1, 2)
-        TA(3, 3, "A")
-        V1(2, 2)
-        CT(1, 2, "B")
-        O2(0, 1, 0, S)
-        AB(2, 3)
-        D2(0, 1)
         O2(0, 0, 1, S)
-        PR(5, 1)
-        PR(5, 0)
-        AB(3, 3)
-        M2(0, 0, 0, 1)
-        O2(0, 0, 0, S)
-        V1(2, 3)
-        CQ(3, 0)
-        V1(3, 3)
         TA(4, 2, "B")
         AB(4, 2)
-        TA(3, 2, "A")
-        PR(2, 3)
-        CT(0, 2, "A")
-        AB(3, 2)
-        CC(0, 2, S)
-        CC(1, 2, S)
-        CT(5, 0, "B")
-        MT(1, 2, "C")
-        TA(5, 2, "A")
-        CC(5, 0, S)
-        PR(2, 2)
-        CT(2, 2, "B")
-        V1(4, 2)
-        MC(1, 2, V)
-        AB(5, 2)
-        PR(3, 3)
-        D2(0, 0)
-        M2(1, 0, 0, 0, "B")
-        MQ(1, 2)
-        CQ(5, 0)
-        M2(1, 0, 0, 1)
-        RI(1, 1, S)
-        M2(1, 0, 1, 0, "C")
-        V1(3, 2)
-        CQ(0, 2)
-        CC(2, 2, S)
-        O2(1, 0, 0, S)
-        M2(1, 0, 1, 1)
-        PR(3, 2)
-        V1(5, 2)
-        O2(1, 0, 1, S)
-        TA(5, 3, "B")
-        RI(3, 0, S)
-        CQ(2, 2)
-        D2(1, 0)
-        TA(4, 3, "A")
-        AB(4, 3)
-        SPZ("C")
-        M2(1, 1, 1, 0, "A")
-        PR(4, 2)
-        M2(1, 1, 1, 1)
-        RI(1, 0, S)
-        CQ(1, 2)
-        V1(5, 3)
-        M2(0, 3, 1, 0, "C")
-        M2(0, 3, 1, 1)
-        O2(0, 3, 1, S)
-        O2(1, 1, 1, S)
-        RI(3, 1, V)
-        RI(0, 1, V)
-        RQ(3, 2)
-        RQ(0, 2)
-        M2(1, 1, 0, 0, "B")
+        M2(0, 1, 1, 0, "A")
+        M2(0, 1, 1, 1)
+        V1(1, 3)
+        O2(0, 1, 1, S)
+        PR(1, 2, V)
+        V1(0, 2)
+        PR(1, 3, V)
+        CT(3, 0, "C")
+        CC(3, 0, S)
+        CT(4, 0, "A")
+        CC(4, 0, S)
+        TA(5, 0, "B")
+        AB(5, 0)
+        load_rate(1, 2)
         V1(4, 3)
-        PR(5, 2)
-        AB(5, 3)
-        PR(5, 3)
+        M2(0, 0, 0, 0, "A")
+        PR(0, 2, V)
+        M2(0, 0, 0, 1)
+        O2(0, 0, 0, S)
+        RI(1, 1, S)
+        SPS(1, 1, "B")
+        V1(4, 2)
+        CT(1, 2, "A")
+        CC(1, 2, S)
+        TA(5, 1, "A")
+        AB(5, 1)
+        M2(0, 1, 0, 0, "C")
+        CQ(4, 0)
+        M2(0, 1, 0, 1)
+        O2(0, 1, 0, S)
+        CQ(3, 0)
+        M2(1, 0, 1, 0, "A")
+        TA(2, 3, "B")
+        PR(0, 3, V)
+        AB(2, 3)
+        CT(0, 2, "A")
+        V1(5, 0)
+        M2(1, 0, 0, 0, "A")
+        PR(4, 3, V)
+        D2(0, 0)
+        PR(4, 2, V)
+        TA(2, 2, "B")
+        V1(5, 1)
+        PR(5, 0, V)
+        PR(5, 1, V)
+        RI(4, 1, S)
+        MQ(1, 0)
+        RI(4, 0, V)
+        AB(2, 2)
+        CT(5, 0, "C")
+        V1(2, 3)
+        M2(1, 1, 0, 0, "A")
+        CC(5, 0, S)
+        CC(0, 2, S)
+        TA(3, 2, "B")
+        AB(3, 2)
+        CQ(5, 0)
+        M2(1, 0, 1, 1)
+        M2(1, 1, 1, 0, "C")
+        MQ(0, 0)
+        O2(1, 0, 1, S)
         M2(1, 1, 0, 1)
-        O2(1, 1, 0, S)
-        D2(1, 1)
-        M2(0, 3, 0, 0, "A")
-        M2(0, 3, 0, 1)
-        O2(0, 3, 0, S)
-        CT(3, 2, "C")
-        CC(3, 2, S)
-        M3(0, 3, 2, "B")
-        O3(0, 3, V)
-        D2(0, 3)
-        M3(0, 2, 2, "B")
-        O3(0, 2, S)
-        PR(4, 3)
+        RI(0, 1, S)
+        M2(1, 1, 1, 1)
+        PR(2, 3, V)
+        O2(1, 1, 1, S)
+        RI(1, 0, V)
+        V1(2, 2)
+        D2(0, 1)
+        TA(5, 2, "A")
+        M2(1, 0, 0, 1)
+        O2(1, 0, 0, S)
+        D2(1, 0)
+        TA(3, 3, "A")
+        AB(3, 3)
         RQ(1, 2)
-        D3(0, 3)
-        M2(0, 2, 0, 0, "B")
-        M2(0, 2, 0, 1)
-        O2(0, 2, 0, S)
-        RI(4, 0, S)
-        CT(5, 2, "A")
-        M2(0, 2, 1, 0, "A")
-        M2(0, 2, 1, 1)
-        RI(4, 1, V)
-        O2(0, 2, 1, V)
-        D3(0, 2)
-        M3(0, 0, 2, "A")
-        O3(0, 0, V)
+        O2(1, 1, 0, V)
+        AB(5, 2)
+        TA(5, 3, "B")
         RQ(4, 2)
-        D2(0, 2)
-        CC(5, 2, V)
-        CQ(3, 2)
-        CT(4, 2, "C")
-        CC(4, 2, S)
-        CQ(5, 2)
-        RI(5, 1, S)
-        M3(0, 1, 2, "B")
-        D3(0, 0)
-        M3(1, 0, 2, "A")
+        M3(1, 2, 2, "C")
+        O3(1, 2, S)
+        V1(5, 3)
+        D2(1, 1)
+        M3(1, 3, 2, "A")
+        PR(2, 2, V)
+        CT(2, 2, "A")
+        O3(1, 3, S)
+        AB(5, 3)
+        D3(1, 2)
+        D3(1, 3)
+        V1(3, 2)
+        CC(2, 2, S)
+        M3(1, 0, 2, "B")
         O3(1, 0, S)
         D3(1, 0)
-        M3(1, 3, 2, "B")
-        M3(1, 2, 2, "A")
-        CQ(4, 2)
-        M2(1, 2, 1, 0, "A")
-        RI(5, 0, V)
-        O3(1, 3, S)
-        D3(1, 3)
-        O3(0, 1, S)
-        D3(0, 1)
-        O3(1, 2, S)
-        D3(1, 2)
-        RI(2, 1, V)
-        M2(1, 2, 0, 0, "A")
-        RI(2, 0, V)
-        M2(1, 2, 0, 1)
-        O2(1, 2, 0, S)
-        M2(1, 2, 1, 1)
-        RQ(5, 0)
-        O2(1, 2, 1, S)
-        D2(1, 2)
-        M3(1, 1, 2, "C")
-        RQ(2, 2)
-        M2(1, 3, 0, 0, "B")
-        M2(1, 3, 0, 1)
-        RQ(5, 1)
+        V1(5, 2)
+        CQ(1, 2)
+        M3(1, 1, 2, "B")
+        CQ(0, 2)
+        M2(0, 2, 0, 0, "A")
         O3(1, 1, S)
         D3(1, 1)
-        M3(2, 1, 0, "A")
-        O2(1, 3, 0, S)
-        M3(2, 1, 1)
-        O3(2, 1, V)
-        M3(2, 2, 0, "B")
+        V1(3, 3)
+        CQ(2, 2)
+        M2(0, 3, 1, 0, "A")
+        M2(0, 3, 1, 1)
+        M2(0, 2, 0, 1)
+        PR(3, 2, V)
+        SPZ("B")
+        PR(3, 3, V)
+        M2(0, 3, 0, 0, "B")
+        PR(5, 2, V)
+        RI(3, 0, V)
+        RI(3, 1, V)
+        RI(0, 0, S)
+        O2(0, 3, 1, S)
+        M2(0, 3, 0, 1)
+        O2(0, 3, 0, S)
+        RQ(0, 2)
+        M2(0, 2, 1, 0, "B")
+        M2(0, 2, 1, 1)
+        O2(0, 2, 1, S)
+        RQ(3, 2)
+        RI(2, 1, V)
+        D2(0, 3)
+        SPS(0, 1, "C")
+        CT(4, 2, "B")
+        O2(0, 2, 0, S)
+        PR(5, 3, V)
+        CT(3, 2, "B")
+        CC(3, 2, S)
+        CQ(3, 2)
+        CC(4, 2, S)
+        CQ(4, 2)
+        RI(2, 0, V)
+        M3(0, 1, 2, "B")
+        O3(0, 1, S)
+        RI(5, 0, V)
+        M3(0, 2, 2, "A")
+        M3(0, 0, 2, "A")
+        O3(0, 0, S)
+        CT(5, 2, "C")
+        D2(0, 2)
+        M2(1, 3, 0, 0, "B")
+        CC(5, 2, S)
+        CQ(5, 2)
+        D3(0, 1)
+        M3(0, 3, 2, "B")
+        M2(1, 3, 1, 0, "A")
+        SPS(0, 1, "A")
+        M2(1, 3, 0, 1)
+        O3(0, 2, S)
+        RI(5, 1, S)
+        O3(0, 3, V)
+        RQ(2, 2)
+        D3(0, 0)
+        M2(1, 3, 1, 1)
+        M2(1, 2, 1, 0, "B")
+        D3(0, 2)
+        M2(1, 2, 1, 1)
+        O2(1, 3, 1, S)
+        D3(0, 3)
+        O2(1, 3, 0, V)
+        RQ(5, 0)
+        M3(2, 0, 0, "C")
+        D2(1, 3)
+        RQ(5, 1)
+        M3(2, 0, 1)
+        O3(2, 0, S)
+        M3(2, 2, 0, "A")
         M3(2, 2, 1)
-        D3(2, 1)
+        D3(2, 0)
         O3(2, 2, V)
         D3(2, 2)
-        M2(1, 3, 1, 0, "C")
-        M2(1, 3, 1, 1)
-        O2(1, 3, 1, S)
-        D2(1, 3)
-        M3(2, 0, 0, "A")
-        M3(2, 0, 1)
-        O3(2, 0, V)
-        D3(2, 0)
-        SPZ("B")
-        M3(2, 3, 0, "C")
+        M2(1, 2, 0, 0, "B")
+        M2(1, 2, 0, 1)
+        O2(1, 2, 1, V)
+        M3(2, 3, 0, "A")
         M3(2, 3, 1)
+        M3(2, 1, 0, "C")
+        M3(2, 1, 1)
+        O2(1, 2, 0, S)
+        D2(1, 2)
+        O3(2, 1, S)
         O3(2, 3, V)
         D3(2, 3)
+        SPS(1, 1, "B")
+        D3(2, 1)
+        SPZ("B")

@@ -213,11 +213,16 @@ def tile_crystal_slip_rates_s8_kernel(
                 mm(ps[:], sig_codes[:, h, g, c], sig_sc[:, h, g, c], sch_codes[:, g, n], sch_sc[:, g, n], g == 0, g == 1)
             tau[(u, t)] = ps
 
+        def even_odd(cols, natural):
+            if natural:
+                return cols.rearrange("p (i u e) -> p u i e", u=2, e=2)
+            return cols.rearrange("p (u i e) -> p u i e", u=2, e=2)
+
         def AB(u, t):
             k = (u, t // 2)
             if k not in a_sb:
                 a_sb[k] = work.tile([P, 2, B], F32, name="a_sb", tag="a_sb", bufs=3)
-            S.activation(out=a_sb[k][:, t % 2, :], in_=tau[(u, t)][:], func=ABS)
+            S.activation(out=even_odd(a_sb[k][:, t % 2, :], False), in_=even_odd(tau[(u, t)][:], True), func=ABS)
 
         def V1(u, t):
             k = (u, t // 2)
@@ -225,22 +230,17 @@ def tile_crystal_slip_rates_s8_kernel(
             if k not in w_sb:
                 w_sb[k] = work.tile([P, 2, B], F32, name="w_sb", tag="w_sb", bufs=2)
             V.tensor_tensor(
-                out=w_sb[k][:, t % 2, :],
-                in0=tau[(u, t)][:],
-                in1=rate_sb[:, h, t, nb * B : nb * B + B],
+                out=even_odd(w_sb[k][:, t % 2, :], False),
+                in0=even_odd(tau[(u, t)][:], True),
+                in1=even_odd(rate_sb[:, h, t, nb * B : nb * B + B], True),
                 op=MULT,
             )
 
-        def PR(u, t, eng):
-            k = (u, t // 2)
+        def PR(u, t0, eng):
+            k = (u, t0 // 2)
             if u not in slip:
                 slip[u] = work.tile([P, 4, B], BF16, name="slip", tag="slip", bufs=6, align_bytes=64)
-            eng.tensor_tensor(
-                out=slip[u][:, t, :].rearrange("p (u i e) -> p u i e", u=2, e=2),
-                in0=w_sb[k][:, t % 2, :].rearrange("p (i u e) -> p u i e", u=2, e=2),
-                in1=a_sb[k][:, t % 2, :].rearrange("p (i u e) -> p u i e", u=2, e=2),
-                op=MULT,
-            )
+            eng.tensor_tensor(out=slip[u][:, t0 : t0 + 2, :], in0=w_sb[k][:], in1=a_sb[k][:], op=MULT)
 
         def CT(u, t0, tag):
             turn_pe(("c", u, t0), slip[u][:, t0 : t0 + 2, :], 0, 1, tag)
@@ -321,358 +321,346 @@ def tile_crystal_slip_rates_s8_kernel(
             tc.manual_schedule(engines={mybir.EngineType.PE, mybir.EngineType.Activation, mybir.EngineType.DVE, mybir.EngineType.SP, mybir.EngineType.Pool})
         )
         load_scale()
-        SPZ("A")
         load_bytes(0, 2)
         W(0, 0, 2, V)
-        W(0, 2, 3, V)
-        W(0, 0, 3, V)
-        SPW(0, 0, 3, "B")
         W(0, 2, 2, V)
-        W(0, 1, 3, S)
-        W(0, 1, 2, S)
-        SPZ("B")
+        W(0, 2, 3, V)
+        W(0, 1, 3, V)
         load_bytes(0, 0)
-        W(0, 0, 1, V)
-        W(0, 1, 0, S)
-        W(0, 0, 0, V)
+        W(0, 2, 1, V)
         W(0, 2, 0, V)
-        I(0, 0, V)
-        W(0, 1, 1, S)
-        SPZ("B")
-        load_bytes(1, 0)
-        W(0, 2, 1, S)
-        SPZ("A")
+        W(0, 1, 2, S)
+        W(0, 0, 3, S)
+        SPW(0, 0, 3, "C")
+        W(0, 0, 0, S)
+        W(0, 1, 0, V)
+        SPW(0, 0, 3, "B")
         I(0, 2, V)
-        Q(0, 0)
-        SPW(0, 0, 3, "A")
-        I(0, 1, S)
-        W(1, 0, 1, S)
-        SPZ("B")
+        W(0, 0, 1, S)
+        I(0, 0, S)
+        load_sigma(1, 0)
+        ST(1, 1, 0, "B")
+        SC(1, 1, 0, S)
+        SPZ("A")
+        ST(1, 0, 0, "B")
+        SC(1, 0, 0, S)
+        W(0, 1, 1, V)
+        Q(0, 2)
+        load_bytes(1, 0)
+        W(1, 1, 1, S)
+        I(0, 1, V)
+        SPZ("C")
+        W(1, 1, 0, V)
         load_sigma(0, 0)
         ST(0, 1, 0, "A")
         SPZ("B")
-        ST(0, 0, 0, "A")
-        load_bytes(1, 2)
-        W(1, 1, 2, S)
-        Q(0, 2)
-        W(1, 2, 2, V)
-        W(1, 0, 3, V)
-        SPW(1, 0, 3, "B")
-        load_sigma(1, 0)
-        Q(0, 1)
-        SPW(1, 0, 3, "B")
-        W(1, 0, 0, V)
-        W(1, 1, 1, V)
-        ST(1, 0, 0, "A")
-        SPZ("B")
-        W(1, 2, 1, S)
-        W(1, 1, 0, V)
         SC(0, 1, 0, S)
-        ST(1, 1, 0, "C")
-        W(1, 1, 3, V)
-        load_sigma(1, 2)
-        ST(1, 0, 2, "B")
-        SQ(0, 1, 0)
-        I(1, 1, V)
-        SPI(1, 1, "A")
-        W(1, 0, 2, S)
-        I(1, 0, V)
-        W(1, 2, 3, S)
-        SC(0, 0, 0, S)
-        SQ(0, 0, 0)
-        SC(1, 0, 0, S)
-        SC(1, 1, 0, S)
-        W(1, 2, 0, S)
-        Q(1, 0)
-        TA(0, 0, "A")
-        Q(1, 1)
-        TA(1, 1, "C")
-        SQ(1, 0, 0)
-        load_rate(0, 0)
-        V1(0, 0)
-        V1(1, 1)
-        TA(0, 1, "B")
-        V1(0, 1)
-        SPI(1, 0, "A")
+        ST(0, 0, 0, "B")
+        Q(0, 0)
+        load_bytes(1, 2)
         SQ(1, 1, 0)
-        TA(1, 0, "A")
-        SC(1, 0, 2, S)
-        I(1, 2, S)
-        V1(1, 0)
-        Q(1, 2)
-        AB(0, 0)
-        PR(0, 0, V)
+        W(1, 1, 3, V)
         load_sigma(0, 2)
-        AB(0, 1)
-        ST(0, 0, 2, "B")
-        PR(0, 1, V)
-        AB(1, 1)
-        AB(1, 0)
-        SQ(1, 0, 2)
+        SQ(1, 0, 0)
+        ST(0, 0, 2, "A")
+        Q(0, 1)
+        load_sigma(1, 2)
+        W(1, 2, 1, V)
+        W(1, 1, 2, S)
+        ST(0, 1, 2, "C")
+        I(1, 1, V)
+        SC(0, 0, 0, S)
+        W(1, 0, 1, V)
+        Q(1, 1)
+        W(1, 2, 0, S)
+        SQ(0, 0, 0)
+        W(1, 0, 0, S)
+        load_rate(1, 0)
+        W(1, 2, 3, V)
+        W(1, 0, 2, S)
+        SPI(1, 1, "B")
+        W(1, 0, 3, S)
+        W(1, 2, 2, S)
+        SQ(0, 1, 0)
         SC(0, 0, 2, S)
-        ST(1, 1, 2, "A")
-        PR(1, 0, V)
-        TA(2, 1, "B")
-        ST(0, 1, 2, "A")
-        PR(1, 1, V)
+        load_rate(0, 0)
+        I(1, 0, V)
+        SPW(1, 0, 3, "B")
         SQ(0, 0, 2)
-        load_rows(("m", 2), mem, 2)
-        MT(0, 2, "B")
-        AB(2, 1)
-        V1(2, 1)
+        TA(1, 0, "A")
         SC(0, 1, 2, S)
         SQ(0, 1, 2)
-        MC(0, 2, S)
+        TA(1, 1, "C")
+        Q(1, 0)
+        V1(1, 1)
+        TA(0, 1, "A")
+        V1(1, 0)
+        V1(0, 1)
+        SPZ("B")
+        TA(0, 0, "B")
+        I(1, 2, S)
+        AB(1, 1)
+        AB(1, 0)
+        TA(3, 0, "A")
+        V1(0, 0)
+        AB(0, 1)
+        AB(0, 0)
+        Q(1, 2)
+        PR(1, 0, V)
         TA(3, 1, "A")
-        AB(3, 1)
-        TA(3, 0, "C")
-        AB(3, 0)
-        TA(2, 0, "B")
-        SC(1, 1, 2, S)
-        PR(2, 1, V)
-        CT(1, 0, "A")
-        V1(2, 0)
-        load_rate(1, 0)
-        V1(3, 0)
-        MT(1, 2, "B")
-        SQ(1, 1, 2)
-        CC(1, 0, S)
-        SPI(1, 1, "B")
+        load_rate(0, 2)
+        ST(1, 0, 2, "B")
+        SC(1, 0, 2, S)
         V1(3, 1)
+        AB(3, 0)
+        load_rows(("m", 0), mem, 0)
+        load_back()
+        TA(2, 1, "A")
+        AB(2, 1)
+        PR(0, 0, V)
+        SPZ("B")
+        CT(1, 0, "B")
+        SQ(1, 0, 2)
+        CC(1, 0, S)
+        TA(2, 3, "B")
+        V1(3, 0)
+        AB(2, 3)
+        TA(2, 0, "B")
+        AB(3, 1)
+        CT(0, 0, "A")
+        V1(2, 0)
+        V1(2, 1)
+        SPS(0, 1, "C")
         AB(2, 0)
-        PR(2, 0, V)
         PR(3, 0, V)
+        TA(2, 2, "A")
+        ST(1, 1, 2, "B")
+        AB(2, 2)
+        CQ(1, 0)
+        SC(1, 1, 2, S)
+        MT(0, 0, "C")
+        MC(0, 0, S)
+        TA(1, 2, "A")
+        CC(0, 0, S)
+        AB(1, 2)
+        load_rows(("m", 2), mem, 2)
+        V1(2, 3)
+        MT(1, 2, "A")
+        MC(1, 2, S)
+        SPW(1, 0, 3, "C")
+        load_rate(1, 2)
+        PR(2, 0, V)
+        TA(1, 3, "A")
+        AB(1, 3)
+        CT(2, 0, "B")
+        CC(2, 0, S)
+        MQ(0, 0)
+        MT(1, 0, "B")
+        V1(2, 2)
+        MC(1, 0, S)
+        V1(1, 2)
+        PR(2, 2, V)
+        V1(1, 3)
+        TA(4, 1, "A")
+        AB(4, 1)
         TA(4, 0, "A")
         AB(4, 0)
-        load_rows(("m", 0), mem, 0)
-        MC(1, 2, S)
-        MQ(1, 2)
-        TA(4, 1, "C")
-        MQ(0, 2)
-        AB(4, 1)
-        PR(3, 1, V)
-        CT(0, 0, "B")
-        CC(0, 0, S)
-        MT(1, 0, "A")
-        V1(4, 0)
-        V1(4, 1)
-        TA(1, 2, "A")
-        AB(1, 2)
-        TA(1, 3, "A")
-        MC(1, 0, S)
-        CT(2, 0, "B")
-        load_rate(0, 2)
-        MT(0, 0, "B")
-        CC(2, 0, S)
-        load_back()
-        MC(0, 0, S)
-        CQ(1, 0)
-        TA(0, 3, "B")
-        CQ(0, 0)
-        PR(4, 0, V)
-        TA(0, 2, "A")
-        CQ(2, 0)
-        AB(0, 3)
-        AB(0, 2)
-        AB(1, 3)
-        PR(4, 1, V)
-        V1(1, 2)
-        V1(0, 3)
-        TA(4, 3, "A")
-        SPI(1, 0, "C")
-        AB(4, 3)
-        M2(0, 0, 1, 0, "B")
-        M2(0, 0, 1, 1)
-        O2(0, 0, 1, S)
-        TA(4, 2, "B")
-        AB(4, 2)
-        M2(0, 1, 1, 0, "A")
-        M2(0, 1, 1, 1)
-        V1(1, 3)
-        O2(0, 1, 1, S)
+        SQ(1, 1, 2)
         PR(1, 2, V)
-        V1(0, 2)
-        PR(1, 3, V)
+        CQ(0, 0)
+        TA(0, 3, "A")
         CT(3, 0, "C")
         CC(3, 0, S)
-        CT(4, 0, "A")
-        CC(4, 0, S)
-        TA(5, 0, "B")
-        AB(5, 0)
-        load_rate(1, 2)
-        V1(4, 3)
-        M2(0, 0, 0, 0, "A")
+        V1(4, 1)
+        AB(0, 3)
+        TA(0, 2, "B")
+        MT(0, 2, "B")
+        V1(4, 0)
+        CT(1, 2, "C")
+        TA(5, 0, "A")
+        AB(0, 2)
+        CC(1, 2, S)
+        V1(0, 3)
+        CQ(2, 0)
+        RI(1, 1, S)
+        TA(5, 1, "A")
+        V1(0, 2)
+        CQ(3, 0)
+        MC(0, 2, S)
+        PR(4, 0, V)
+        MQ(1, 2)
+        M2(0, 0, 1, 0, "B")
+        CT(2, 2, "C")
+        V1(5, 0)
+        AB(5, 1)
+        V1(5, 1)
+        SPI(1, 0, "B")
+        M2(0, 0, 1, 1)
+        MQ(1, 0)
+        O2(0, 0, 1, S)
         PR(0, 2, V)
+        TA(4, 3, "A")
+        AB(4, 3)
+        CC(2, 2, S)
+        M2(0, 0, 0, 0, "B")
+        TA(3, 2, "B")
+        AB(5, 0)
         M2(0, 0, 0, 1)
         O2(0, 0, 0, S)
-        RI(1, 1, S)
-        SPS(1, 1, "B")
-        V1(4, 2)
-        CT(1, 2, "A")
-        CC(1, 2, S)
-        TA(5, 1, "A")
-        AB(5, 1)
-        M2(0, 1, 0, 0, "C")
-        CQ(4, 0)
-        M2(0, 1, 0, 1)
-        O2(0, 1, 0, S)
-        CQ(3, 0)
-        M2(1, 0, 1, 0, "A")
-        TA(2, 3, "B")
-        PR(0, 3, V)
-        AB(2, 3)
-        CT(0, 2, "A")
-        V1(5, 0)
-        M2(1, 0, 0, 0, "A")
-        PR(4, 3, V)
-        D2(0, 0)
-        PR(4, 2, V)
-        TA(2, 2, "B")
-        V1(5, 1)
         PR(5, 0, V)
-        PR(5, 1, V)
-        RI(4, 1, S)
-        MQ(1, 0)
-        RI(4, 0, V)
-        AB(2, 2)
-        CT(5, 0, "C")
-        V1(2, 3)
-        M2(1, 1, 0, 0, "A")
-        CC(5, 0, S)
-        CC(0, 2, S)
-        TA(3, 2, "B")
+        TA(4, 2, "A")
+        AB(4, 2)
+        V1(4, 3)
+        V1(3, 2)
+        RI(1, 0, S)
+        M2(0, 1, 0, 0, "A")
+        M2(0, 1, 0, 1)
+        CT(4, 0, "B")
+        V1(4, 2)
+        CC(4, 0, S)
+        CQ(4, 0)
+        PR(4, 2, V)
+        O2(0, 1, 0, S)
+        TA(3, 3, "B")
         AB(3, 2)
-        CQ(5, 0)
-        M2(1, 0, 1, 1)
-        M2(1, 1, 1, 0, "C")
-        MQ(0, 0)
-        O2(1, 0, 1, S)
-        M2(1, 1, 0, 1)
-        RI(0, 1, S)
-        M2(1, 1, 1, 1)
-        PR(2, 3, V)
-        O2(1, 1, 1, S)
-        RI(1, 0, V)
-        V1(2, 2)
-        D2(0, 1)
+        CT(0, 2, "A")
+        CC(0, 2, S)
+        RQ(1, 2)
+        SPI(1, 0, "C")
+        CQ(0, 2)
+        SPI(1, 1, "C")
+        CT(5, 0, "C")
+        CC(5, 0, S)
         TA(5, 2, "A")
+        AB(5, 2)
+        SPS(1, 1, "A")
+        M2(0, 1, 1, 0, "A")
+        M2(0, 1, 1, 1)
+        V1(5, 2)
+        M2(1, 0, 1, 0, "C")
+        O2(0, 1, 1, S)
+        MQ(0, 2)
+        M2(1, 0, 0, 0, "A")
+        D2(0, 0)
+        CQ(5, 0)
+        SPZ("A")
+        RI(4, 1, S)
+        D2(0, 1)
+        RI(4, 0, V)
+        M2(1, 1, 1, 0, "A")
+        AB(3, 3)
+        M2(1, 0, 1, 1)
+        O2(1, 0, 1, S)
         M2(1, 0, 0, 1)
         O2(1, 0, 0, S)
         D2(1, 0)
-        TA(3, 3, "A")
-        AB(3, 3)
-        RQ(1, 2)
-        O2(1, 1, 0, V)
-        AB(5, 2)
-        TA(5, 3, "B")
-        RQ(4, 2)
-        M3(1, 2, 2, "C")
-        O3(1, 2, S)
-        V1(5, 3)
-        D2(1, 1)
-        M3(1, 3, 2, "A")
-        PR(2, 2, V)
-        CT(2, 2, "A")
-        O3(1, 3, S)
-        AB(5, 3)
-        D3(1, 2)
-        D3(1, 3)
-        V1(3, 2)
-        CC(2, 2, S)
-        M3(1, 0, 2, "B")
-        O3(1, 0, S)
-        D3(1, 0)
-        V1(5, 2)
         CQ(1, 2)
-        M3(1, 1, 2, "B")
-        CQ(0, 2)
-        M2(0, 2, 0, 0, "A")
-        O3(1, 1, S)
-        D3(1, 1)
-        V1(3, 3)
         CQ(2, 2)
-        M2(0, 3, 1, 0, "A")
-        M2(0, 3, 1, 1)
-        M2(0, 2, 0, 1)
-        PR(3, 2, V)
-        SPZ("B")
-        PR(3, 3, V)
+        TA(5, 3, "B")
         M2(0, 3, 0, 0, "B")
-        PR(5, 2, V)
-        RI(3, 0, V)
-        RI(3, 1, V)
-        RI(0, 0, S)
-        O2(0, 3, 1, S)
+        AB(5, 3)
+        RQ(4, 2)
+        M3(1, 3, 2, "C")
+        O3(1, 3, S)
+        V1(3, 3)
+        D3(1, 3)
+        RI(0, 0, V)
+        V1(5, 3)
+        M3(1, 1, 2, "A")
+        O3(1, 1, S)
         M2(0, 3, 0, 1)
+        D3(1, 1)
+        M2(1, 1, 1, 1)
+        M2(1, 1, 0, 0, "B")
+        M2(1, 1, 0, 1)
+        PR(3, 2, V)
+        RI(0, 1, V)
+        M2(0, 3, 1, 0, "A")
+        O2(1, 1, 1, S)
         O2(0, 3, 0, S)
+        M2(0, 3, 1, 1)
+        O2(0, 3, 1, V)
+        RI(3, 0, V)
+        O2(1, 1, 0, S)
+        D2(1, 1)
         RQ(0, 2)
-        M2(0, 2, 1, 0, "B")
-        M2(0, 2, 1, 1)
-        O2(0, 2, 1, S)
-        RQ(3, 2)
-        RI(2, 1, V)
+        M3(1, 2, 2, "C")
         D2(0, 3)
+        RI(3, 1, S)
+        RQ(3, 2)
+        M2(0, 2, 0, 0, "B")
+        O3(1, 2, S)
+        M3(1, 0, 2, "A")
+        O3(1, 0, S)
+        D3(1, 2)
+        D3(1, 0)
+        M2(0, 2, 1, 0, "A")
+        RI(2, 1, S)
+        M2(0, 2, 1, 1)
         SPS(0, 1, "C")
-        CT(4, 2, "B")
-        O2(0, 2, 0, S)
-        PR(5, 3, V)
-        CT(3, 2, "B")
-        CC(3, 2, S)
-        CQ(3, 2)
-        CC(4, 2, S)
-        CQ(4, 2)
-        RI(2, 0, V)
-        M3(0, 1, 2, "B")
-        O3(0, 1, S)
-        RI(5, 0, V)
+        PR(5, 2, V)
         M3(0, 2, 2, "A")
-        M3(0, 0, 2, "A")
-        O3(0, 0, S)
-        CT(5, 2, "C")
-        D2(0, 2)
-        M2(1, 3, 0, 0, "B")
-        CC(5, 2, S)
-        CQ(5, 2)
-        D3(0, 1)
-        M3(0, 3, 2, "B")
-        M2(1, 3, 1, 0, "A")
-        SPS(0, 1, "A")
-        M2(1, 3, 0, 1)
-        O3(0, 2, S)
-        RI(5, 1, S)
-        O3(0, 3, V)
-        RQ(2, 2)
-        D3(0, 0)
-        M2(1, 3, 1, 1)
-        M2(1, 2, 1, 0, "B")
-        D3(0, 2)
-        M2(1, 2, 1, 1)
-        O2(1, 3, 1, S)
+        M3(0, 3, 2, "A")
+        O3(0, 3, S)
+        O3(0, 2, V)
         D3(0, 3)
-        O2(1, 3, 0, V)
+        D3(0, 2)
+        M2(0, 2, 0, 1)
+        RI(2, 0, V)
+        O2(0, 2, 1, S)
+        SPZ("C")
+        O2(0, 2, 0, V)
+        CT(3, 2, "B")
+        RQ(2, 2)
+        D2(0, 2)
+        CT(4, 2, "B")
+        CT(5, 2, "A")
+        RI(5, 1, V)
+        M3(0, 0, 2, "A")
+        RI(5, 0, S)
+        O3(0, 0, S)
+        D3(0, 0)
+        M3(0, 1, 2, "A")
+        CC(4, 2, S)
+        O3(0, 1, S)
+        D3(0, 1)
         RQ(5, 0)
-        M3(2, 0, 0, "C")
-        D2(1, 3)
         RQ(5, 1)
-        M3(2, 0, 1)
-        O3(2, 0, S)
-        M3(2, 2, 0, "A")
-        M3(2, 2, 1)
-        D3(2, 0)
-        O3(2, 2, V)
-        D3(2, 2)
-        M2(1, 2, 0, 0, "B")
-        M2(1, 2, 0, 1)
-        O2(1, 2, 1, V)
-        M3(2, 3, 0, "A")
-        M3(2, 3, 1)
-        M3(2, 1, 0, "C")
+        CC(3, 2, V)
+        CQ(3, 2)
+        CQ(4, 2)
+        M3(2, 1, 0, "B")
+        M3(2, 3, 0, "C")
         M3(2, 1, 1)
-        O2(1, 2, 0, S)
-        D2(1, 2)
         O3(2, 1, S)
+        D3(2, 1)
+        CC(5, 2, S)
+        M3(2, 3, 1)
         O3(2, 3, V)
         D3(2, 3)
-        SPS(1, 1, "B")
-        D3(2, 1)
+        M3(2, 0, 0, "A")
+        M3(2, 0, 1)
+        O3(2, 0, S)
+        D3(2, 0)
+        M2(1, 2, 1, 0, "B")
+        CQ(5, 2)
+        M2(1, 2, 0, 0, "B")
+        M2(1, 2, 0, 1)
+        M2(1, 2, 1, 1)
+        O2(1, 2, 1, V)
+        O2(1, 2, 0, S)
+        M2(1, 3, 0, 0, "B")
+        M3(2, 2, 0, "A")
+        M3(2, 2, 1)
+        O3(2, 2, S)
+        M2(1, 3, 1, 0, "C")
+        M2(1, 3, 1, 1)
+        O2(1, 3, 1, V)
+        D2(1, 2)
+        M2(1, 3, 0, 1)
+        O2(1, 3, 0, S)
         SPZ("B")
+        SPZ("A")
+        D3(2, 2)
+        D2(1, 3)
+        SPS(1, 1, "A")

@@ -68,9 +68,9 @@ def tile_crystal_slip_rates_s8_kernel(
         def load_sigma(h, t0):
             load_rows(("s", h, t0), sigma[h * B : (h + 1) * B, :], t0)
 
-        def load_bytes(g, t0):
+        def load_bytes(g, t):
             v = schmid_bytes[g * B : (g + 1) * B, :].rearrange("(p t) n -> p t n", t=4)
-            nc.sync.dma_start(out=byt[:, g, t0 : t0 + 2], in_=v[:, t0 : t0 + 2, :])
+            nc.sync.dma_start(out=byt[:, g, t], in_=v[:, t, :])
 
         def load_rate(h, t0):
             v = rate[h * B : (h + 1) * B, :].rearrange("(p t) n -> p t n", t=4)
@@ -90,12 +90,13 @@ def tile_crystal_slip_rates_s8_kernel(
         def copy(eng, out, in_):
             if eng is S:
                 S.copy(out=out, in_=in_)
-            elif eng is G:
-                G.tensor_scalar(out=out, in0=in_, scalar1=1.0, scalar2=0.0, op0=MULT, op1=ADD)
             else:
                 V.tensor_copy(out=out, in_=in_)
 
         def weave(eng, out, in_):
+            if eng is G:
+                G.tensor_scalar(out=out, in0=in_.rearrange("p t c -> p c t"), scalar1=1.0, scalar2=0.0, op0=MULT, op1=ADD)
+                return
             copy(eng, out.rearrange("p (c i) t -> p c t i", i=4), in_.rearrange("p t (c i) -> p c t i", i=4))
 
         def bank(tag, shape):
@@ -256,7 +257,7 @@ def tile_crystal_slip_rates_s8_kernel(
         def RI(u, p, eng):
             key = ("r", u)
             new_grp(key)
-            c = slice(256 * p, 256 * (p + 1))
+            c = slice(*((0, 256), (256, 384), (384, 512))[p])
             weave(eng, grp[key][:, c, :], slip[u][:, :, c])
 
         def RQ(u, p):
@@ -291,8 +292,9 @@ def tile_crystal_slip_rates_s8_kernel(
                 osb[(h, t)] = work.tile([P, C], F32, name="osb", tag="osb", bufs=3)
             copy(eng, osb[(h, t)][:, c * B : (c + 1) * B], st2[(h, t, c)][:])
 
-        def D2(h, t):
-            nc.sync.dma_start(out=strain_v[h, :, t, :], in_=osb[(h, t)][:])
+        def D2(h, t, c):
+            cols = slice(0, C) if c == 2 else slice(c * B, (c + 1) * B)
+            nc.sync.dma_start(out=strain_v[h, :, t, cols], in_=osb[(h, t)][:, cols])
 
         def M3(nb, s, p, tag=None):
             key = (nb, s)
@@ -320,347 +322,359 @@ def tile_crystal_slip_rates_s8_kernel(
         ctx.enter_context(
             tc.manual_schedule(engines={mybir.EngineType.PE, mybir.EngineType.Activation, mybir.EngineType.DVE, mybir.EngineType.SP, mybir.EngineType.Pool})
         )
-        load_scale()
+        SPZ("B")
         load_bytes(0, 2)
-        W(0, 0, 2, V)
-        W(0, 2, 2, V)
-        W(0, 2, 3, V)
-        W(0, 1, 3, V)
-        load_bytes(0, 0)
-        W(0, 2, 1, V)
-        W(0, 2, 0, V)
-        W(0, 1, 2, S)
-        W(0, 0, 3, S)
-        SPW(0, 0, 3, "C")
-        W(0, 0, 0, S)
-        W(0, 1, 0, V)
-        SPW(0, 0, 3, "B")
-        I(0, 2, V)
-        W(0, 0, 1, S)
-        I(0, 0, S)
-        load_sigma(1, 0)
-        ST(1, 1, 0, "B")
-        SC(1, 1, 0, S)
-        SPZ("A")
-        ST(1, 0, 0, "B")
-        SC(1, 0, 0, S)
-        W(0, 1, 1, V)
-        Q(0, 2)
-        load_bytes(1, 0)
-        W(1, 1, 1, S)
-        I(0, 1, V)
+        SPZ("B")
         SPZ("C")
-        W(1, 1, 0, V)
+        load_scale()
+        W(0, 2, 2, V)
+        W(0, 0, 2, V)
+        SPZ("C")
+        W(0, 1, 2, S)
+        load_bytes(0, 0)
+        W(0, 1, 0, V)
+        W(0, 0, 0, S)
+        W(0, 2, 0, V)
+        load_bytes(0, 3)
+        SPZ("B")
+        W(0, 0, 3, V)
+        W(0, 1, 3, S)
+        SPW(0, 0, 3, "A")
+        load_bytes(0, 1)
         load_sigma(0, 0)
-        ST(0, 1, 0, "A")
-        SPZ("B")
-        SC(0, 1, 0, S)
-        ST(0, 0, 0, "B")
-        Q(0, 0)
-        load_bytes(1, 2)
-        SQ(1, 1, 0)
-        W(1, 1, 3, V)
-        load_sigma(0, 2)
-        SQ(1, 0, 0)
-        ST(0, 0, 2, "A")
-        Q(0, 1)
-        load_sigma(1, 2)
-        W(1, 2, 1, V)
-        W(1, 1, 2, S)
-        ST(0, 1, 2, "C")
-        I(1, 1, V)
-        SC(0, 0, 0, S)
-        W(1, 0, 1, V)
-        Q(1, 1)
-        W(1, 2, 0, S)
-        SQ(0, 0, 0)
-        W(1, 0, 0, S)
-        load_rate(1, 0)
+        W(0, 2, 3, V)
+        SPW(0, 0, 3, "B")
+        W(0, 0, 1, V)
+        W(0, 2, 1, V)
+        I(0, 0, V)
+        I(0, 2, V)
+        W(0, 1, 1, S)
+        I(0, 1, S)
+        load_bytes(1, 3)
         W(1, 2, 3, V)
-        W(1, 0, 2, S)
-        SPI(1, 1, "B")
-        W(1, 0, 3, S)
-        W(1, 2, 2, S)
+        load_bytes(1, 0)
+        W(1, 0, 0, V)
+        load_bytes(1, 2)
+        W(1, 1, 2, V)
+        SPZ("A")
+        Q(0, 0)
+        W(1, 2, 0, V)
+        ST(0, 1, 0, "B")
+        SC(0, 1, 0, S)
         SQ(0, 1, 0)
-        SC(0, 0, 2, S)
-        load_rate(0, 0)
+        W(1, 1, 3, S)
+        W(1, 0, 3, V)
+        Q(0, 2)
+        load_bytes(1, 1)
+        W(1, 0, 1, S)
+        W(1, 0, 2, S)
         I(1, 0, V)
-        SPW(1, 0, 3, "B")
-        SQ(0, 0, 2)
-        TA(1, 0, "A")
-        SC(0, 1, 2, S)
-        SQ(0, 1, 2)
-        TA(1, 1, "C")
+        W(1, 1, 0, S)
+        ST(0, 0, 0, "B")
+        load_sigma(1, 0)
+        ST(1, 1, 0, "A")
+        W(1, 1, 1, S)
+        I(1, 1, V)
+        ST(1, 0, 0, "A")
         Q(1, 0)
-        V1(1, 1)
+        SC(0, 0, 0, S)
+        SQ(0, 0, 0)
+        SC(1, 1, 0, S)
+        SQ(1, 1, 0)
+        Q(0, 1)
+        SPI(1, 0, "C")
+        Q(1, 1)
+        load_rows(("m", 0), mem, 0)
+        SC(1, 0, 0, S)
+        SQ(1, 0, 0)
+        SPZ("C")
+        SPI(1, 0, "B")
+        SPI(1, 1, "C")
+        W(1, 2, 1, S)
         TA(0, 1, "A")
-        V1(1, 0)
+        load_rate(0, 0)
         V1(0, 1)
-        SPZ("B")
-        TA(0, 0, "B")
-        I(1, 2, S)
-        AB(1, 1)
-        AB(1, 0)
-        TA(3, 0, "A")
+        TA(0, 0, "A")
         V1(0, 0)
+        TA(1, 1, "A")
+        SPI(1, 1, "B")
+        V1(1, 1)
+        TA(1, 0, "B")
+        V1(1, 0)
+        W(1, 2, 2, S)
+        I(1, 2, S)
+        Q(1, 2)
         AB(0, 1)
         AB(0, 0)
-        Q(1, 2)
-        PR(1, 0, V)
-        TA(3, 1, "A")
-        load_rate(0, 2)
-        ST(1, 0, 2, "B")
-        SC(1, 0, 2, S)
-        V1(3, 1)
-        AB(3, 0)
-        load_rows(("m", 0), mem, 0)
-        load_back()
-        TA(2, 1, "A")
-        AB(2, 1)
         PR(0, 0, V)
-        SPZ("B")
-        CT(1, 0, "B")
-        SQ(1, 0, 2)
-        CC(1, 0, S)
-        TA(2, 3, "B")
-        V1(3, 0)
-        AB(2, 3)
-        TA(2, 0, "B")
+        AB(1, 0)
+        TA(3, 1, "B")
         AB(3, 1)
-        CT(0, 0, "A")
-        V1(2, 0)
-        V1(2, 1)
-        SPS(0, 1, "C")
-        AB(2, 0)
-        PR(3, 0, V)
-        TA(2, 2, "A")
+        AB(1, 1)
+        load_rate(1, 0)
+        V1(3, 1)
+        load_sigma(0, 2)
+        ST(0, 0, 2, "A")
+        SC(0, 0, 2, S)
+        PR(1, 0, V)
+        load_sigma(1, 2)
+        SQ(0, 0, 2)
+        ST(0, 1, 2, "A")
+        SC(0, 1, 2, S)
+        SQ(0, 1, 2)
+        TA(3, 0, "B")
+        load_rate(0, 2)
+        ST(1, 0, 2, "A")
+        AB(3, 0)
+        V1(3, 0)
         ST(1, 1, 2, "B")
-        AB(2, 2)
-        CQ(1, 0)
         SC(1, 1, 2, S)
-        MT(0, 0, "C")
-        MC(0, 0, S)
-        TA(1, 2, "A")
-        CC(0, 0, S)
-        AB(1, 2)
-        load_rows(("m", 2), mem, 2)
-        V1(2, 3)
-        MT(1, 2, "A")
-        MC(1, 2, S)
-        SPW(1, 0, 3, "C")
-        load_rate(1, 2)
-        PR(2, 0, V)
-        TA(1, 3, "A")
-        AB(1, 3)
-        CT(2, 0, "B")
-        CC(2, 0, S)
-        MQ(0, 0)
-        MT(1, 0, "B")
-        V1(2, 2)
-        MC(1, 0, S)
-        V1(1, 2)
-        PR(2, 2, V)
-        V1(1, 3)
-        TA(4, 1, "A")
-        AB(4, 1)
-        TA(4, 0, "A")
-        AB(4, 0)
         SQ(1, 1, 2)
-        PR(1, 2, V)
+        TA(2, 1, "A")
+        TA(2, 0, "A")
+        CT(0, 0, "C")
+        CT(1, 0, "A")
+        AB(2, 0)
+        V1(2, 1)
+        V1(2, 0)
+        MT(0, 0, "B")
+        PR(3, 0, G)
+        CC(0, 0, V)
         CQ(0, 0)
-        TA(0, 3, "A")
+        SC(1, 0, 2, S)
+        AB(2, 1)
+        load_rows(("m", 2), mem, 2)
+        TA(1, 2, "B")
+        MC(0, 0, S)
+        load_back()
+        AB(1, 2)
+        TA(1, 3, "B")
+        AB(1, 3)
+        MT(0, 2, "A")
+        PR(2, 0, G)
+        MT(1, 2, "B")
+        CC(1, 0, V)
+        MC(0, 2, S)
         CT(3, 0, "C")
         CC(3, 0, S)
-        V1(4, 1)
-        AB(0, 3)
-        TA(0, 2, "B")
-        MT(0, 2, "B")
-        V1(4, 0)
-        CT(1, 2, "C")
-        TA(5, 0, "A")
-        AB(0, 2)
-        CC(1, 2, S)
-        V1(0, 3)
+        V1(1, 2)
+        V1(1, 3)
+        TA(2, 2, "A")
+        AB(2, 2)
+        SPS(0, 1, "A")
+        TA(2, 3, "A")
+        SQ(1, 0, 2)
+        PR(1, 2, V)
+        TA(4, 1, "A")
+        MC(1, 2, S)
+        CT(2, 0, "C")
+        AB(4, 1)
+        V1(2, 3)
+        CQ(1, 0)
+        SPZ("B")
+        CC(2, 0, S)
         CQ(2, 0)
-        RI(1, 1, S)
-        TA(5, 1, "A")
-        V1(0, 2)
-        CQ(3, 0)
-        MC(0, 2, S)
-        PR(4, 0, V)
-        MQ(1, 2)
-        M2(0, 0, 1, 0, "B")
-        CT(2, 2, "C")
-        V1(5, 0)
-        AB(5, 1)
-        V1(5, 1)
-        SPI(1, 0, "B")
-        M2(0, 0, 1, 1)
-        MQ(1, 0)
-        O2(0, 0, 1, S)
-        PR(0, 2, V)
-        TA(4, 3, "A")
-        AB(4, 3)
-        CC(2, 2, S)
+        TA(4, 0, "B")
+        V1(4, 0)
+        V1(2, 2)
         M2(0, 0, 0, 0, "B")
-        TA(3, 2, "B")
-        AB(5, 0)
-        M2(0, 0, 0, 1)
-        O2(0, 0, 0, S)
-        PR(5, 0, V)
-        TA(4, 2, "A")
-        AB(4, 2)
-        V1(4, 3)
-        V1(3, 2)
+        RI(1, 1, G)
         RI(1, 0, S)
-        M2(0, 1, 0, 0, "A")
-        M2(0, 1, 0, 1)
-        CT(4, 0, "B")
-        V1(4, 2)
-        CC(4, 0, S)
-        CQ(4, 0)
-        PR(4, 2, V)
-        O2(0, 1, 0, S)
-        TA(3, 3, "B")
+        AB(2, 3)
+        TA(5, 0, "B")
+        AB(5, 0)
+        SPS(1, 1, "C")
+        CT(1, 2, "C")
+        V1(4, 1)
+        PR(2, 2, V)
+        MT(1, 0, "A")
+        AB(4, 0)
+        MQ(0, 0)
+        TA(5, 1, "A")
+        AB(5, 1)
+        V1(5, 0)
+        M2(0, 0, 0, 1)
+        CC(1, 2, S)
+        TA(0, 3, "A")
+        V1(5, 1)
+        MC(1, 0, S)
+        O2(0, 0, 0, V)
+        RI(1, 2, G)
+        TA(0, 2, "B")
+        AB(0, 2)
+        M2(0, 0, 1, 0, "A")
+        M2(0, 0, 1, 1)
+        PR(4, 0, G)
+        MQ(0, 2)
+        O2(0, 0, 1, V)
+        AB(0, 3)
+        M2(0, 1, 1, 0, "A")
+        TA(3, 2, "A")
         AB(3, 2)
-        CT(0, 2, "A")
-        CC(0, 2, S)
-        RQ(1, 2)
-        SPI(1, 0, "C")
-        CQ(0, 2)
-        SPI(1, 1, "C")
+        V1(0, 2)
+        M2(0, 1, 0, 0, "B")
+        PR(5, 0, G)
+        M2(0, 1, 1, 1)
+        O2(0, 1, 1, S)
+        TA(3, 3, "B")
+        AB(3, 3)
+        M2(0, 1, 0, 1)
+        O2(0, 1, 0, S)
+        TA(4, 2, "B")
+        AB(4, 2)
+        SPW(1, 0, 3, "C")
+        V1(0, 3)
+        load_rate(1, 2)
         CT(5, 0, "C")
         CC(5, 0, S)
-        TA(5, 2, "A")
-        AB(5, 2)
-        SPS(1, 1, "A")
-        M2(0, 1, 1, 0, "A")
-        M2(0, 1, 1, 1)
-        V1(5, 2)
-        M2(1, 0, 1, 0, "C")
-        O2(0, 1, 1, S)
-        MQ(0, 2)
-        M2(1, 0, 0, 0, "A")
-        D2(0, 0)
-        CQ(5, 0)
-        SPZ("A")
-        RI(4, 1, S)
-        D2(0, 1)
-        RI(4, 0, V)
-        M2(1, 1, 1, 0, "A")
-        AB(3, 3)
-        M2(1, 0, 1, 1)
-        O2(1, 0, 1, S)
-        M2(1, 0, 0, 1)
-        O2(1, 0, 0, S)
-        D2(1, 0)
-        CQ(1, 2)
-        CQ(2, 2)
-        TA(5, 3, "B")
-        M2(0, 3, 0, 0, "B")
-        AB(5, 3)
-        RQ(4, 2)
-        M3(1, 3, 2, "C")
-        O3(1, 3, S)
+        PR(0, 2, V)
+        D2(0, 0, 2)
+        CT(4, 0, "B")
+        CQ(3, 0)
+        CT(0, 2, "A")
+        CC(0, 2, S)
+        D2(0, 1, 2)
+        MQ(1, 2)
+        V1(3, 2)
         V1(3, 3)
-        D3(1, 3)
-        RI(0, 0, V)
-        V1(5, 3)
-        M3(1, 1, 2, "A")
-        O3(1, 1, S)
-        M2(0, 3, 0, 1)
-        D3(1, 1)
-        M2(1, 1, 1, 1)
-        M2(1, 1, 0, 0, "B")
-        M2(1, 1, 0, 1)
-        PR(3, 2, V)
-        RI(0, 1, V)
+        CT(2, 2, "A")
+        CC(2, 2, S)
+        RI(0, 1, G)
+        CQ(0, 2)
+        TA(4, 3, "A")
+        TA(5, 3, "A")
+        CQ(1, 2)
         M2(0, 3, 1, 0, "A")
-        O2(1, 1, 1, S)
-        O2(0, 3, 0, S)
-        M2(0, 3, 1, 1)
-        O2(0, 3, 1, V)
-        RI(3, 0, V)
-        O2(1, 1, 0, S)
-        D2(1, 1)
-        RQ(0, 2)
-        M3(1, 2, 2, "C")
-        D2(0, 3)
-        RI(3, 1, S)
-        RQ(3, 2)
         M2(0, 2, 0, 0, "B")
-        O3(1, 2, S)
-        M3(1, 0, 2, "A")
-        O3(1, 0, S)
-        D3(1, 2)
-        D3(1, 0)
-        M2(0, 2, 1, 0, "A")
-        RI(2, 1, S)
-        M2(0, 2, 1, 1)
-        SPS(0, 1, "C")
-        PR(5, 2, V)
-        M3(0, 2, 2, "A")
-        M3(0, 3, 2, "A")
-        O3(0, 3, S)
-        O3(0, 2, V)
-        D3(0, 3)
-        D3(0, 2)
+        PR(3, 2, V)
+        CQ(2, 2)
+        CC(4, 0, S)
+        CQ(4, 0)
+        M2(0, 3, 0, 0, "C")
+        M2(0, 3, 0, 1)
+        M2(0, 3, 1, 1)
         M2(0, 2, 0, 1)
-        RI(2, 0, V)
-        O2(0, 2, 1, S)
-        SPZ("C")
-        O2(0, 2, 0, V)
+        RI(3, 2, G)
+        RI(0, 2, S)
+        V1(4, 2)
+        M2(0, 2, 1, 0, "B")
+        RI(0, 0, S)
+        O2(0, 3, 0, V)
+        O2(0, 3, 1, S)
+        D2(0, 3, 2)
+        M2(0, 2, 1, 1)
+        AB(5, 3)
+        V1(4, 3)
+        AB(4, 3)
+        TA(5, 2, "C")
+        RI(3, 0, V)
+        RQ(0, 2)
+        O2(0, 2, 0, S)
         CT(3, 2, "B")
-        RQ(2, 2)
-        D2(0, 2)
-        CT(4, 2, "B")
-        CT(5, 2, "A")
-        RI(5, 1, V)
-        M3(0, 0, 2, "A")
-        RI(5, 0, S)
-        O3(0, 0, S)
-        D3(0, 0)
+        O2(0, 2, 1, S)
+        D2(0, 2, 2)
+        AB(5, 2)
+        CC(3, 2, S)
+        M2(1, 0, 0, 0, "A")
+        RI(3, 1, G)
+        CQ(5, 0)
+        RQ(3, 2)
+        M2(1, 0, 0, 1)
+        M3(0, 2, 2, "B")
+        O3(0, 2, S)
+        MQ(1, 0)
         M3(0, 1, 2, "A")
-        CC(4, 2, S)
+        O2(1, 0, 0, V)
+        M2(1, 0, 1, 0, "B")
+        M2(1, 0, 1, 1)
         O3(0, 1, S)
+        M3(0, 0, 2, "B")
+        PR(4, 2, V)
+        O2(1, 0, 1, S)
+        D3(0, 2)
+        RI(4, 2, S)
+        RI(4, 0, G)
+        V1(5, 2)
+        M2(1, 1, 0, 0, "B")
         D3(0, 1)
-        RQ(5, 0)
-        RQ(5, 1)
-        CC(3, 2, V)
-        CQ(3, 2)
+        M2(1, 1, 0, 1)
+        V1(5, 3)
+        RI(4, 1, S)
+        O2(1, 1, 0, S)
+        M2(1, 1, 1, 0, "B")
+        M2(1, 1, 1, 1)
+        O2(1, 1, 1, S)
+        M3(0, 3, 2, "A")
+        D2(1, 0, 2)
+        O3(0, 0, V)
+        PR(5, 2, V)
+        CT(5, 2, "B")
+        D3(0, 0)
+        RQ(1, 2)
+        O3(0, 3, S)
+        CT(4, 2, "A")
+        CC(4, 2, S)
+        RQ(4, 2)
+        CC(5, 2, V)
+        D2(1, 1, 2)
+        M3(1, 2, 2, "A")
+        M3(1, 0, 2, "A")
+        O3(1, 2, S)
+        O3(1, 0, S)
+        M3(1, 3, 2, "A")
         CQ(4, 2)
-        M3(2, 1, 0, "B")
-        M3(2, 3, 0, "C")
-        M3(2, 1, 1)
-        O3(2, 1, S)
-        D3(2, 1)
-        CC(5, 2, S)
-        M3(2, 3, 1)
-        O3(2, 3, V)
-        D3(2, 3)
-        M3(2, 0, 0, "A")
-        M3(2, 0, 1)
-        O3(2, 0, S)
-        D3(2, 0)
-        M2(1, 2, 1, 0, "B")
+        CQ(3, 2)
+        D3(0, 3)
+        D3(1, 2)
+        M2(1, 3, 1, 0, "B")
         CQ(5, 2)
+        M2(1, 3, 1, 1)
+        RI(2, 1, G)
+        O3(1, 3, V)
+        D3(1, 0)
+        D3(1, 3)
+        RI(2, 2, S)
+        RI(5, 0, G)
+        RI(5, 2, S)
+        O2(1, 3, 1, V)
+        RI(2, 0, S)
+        RI(5, 1, G)
         M2(1, 2, 0, 0, "B")
         M2(1, 2, 0, 1)
+        D2(1, 3, 1)
+        O2(1, 2, 0, V)
+        M3(1, 1, 2, "B")
+        O3(1, 1, V)
+        D2(1, 2, 0)
+        M2(1, 2, 1, 0, "A")
         M2(1, 2, 1, 1)
-        O2(1, 2, 1, V)
-        O2(1, 2, 0, S)
-        M2(1, 3, 0, 0, "B")
-        M3(2, 2, 0, "A")
-        M3(2, 2, 1)
-        O3(2, 2, S)
-        M2(1, 3, 1, 0, "C")
-        M2(1, 3, 1, 1)
-        O2(1, 3, 1, V)
-        D2(1, 2)
+        O2(1, 2, 1, S)
+        D3(1, 1)
+        M2(1, 3, 0, 0, "A")
+        RQ(2, 2)
         M2(1, 3, 0, 1)
+        D2(1, 2, 1)
+        RQ(5, 0)
         O2(1, 3, 0, S)
+        RQ(5, 1)
+        D2(1, 3, 0)
+        M3(2, 0, 0, "A")
+        M3(2, 0, 1)
+        M3(2, 1, 0, "B")
+        O3(2, 0, S)
+        M3(2, 1, 1)
         SPZ("B")
-        SPZ("A")
+        M3(2, 2, 0, "C")
+        M3(2, 2, 1)
+        M3(2, 3, 0, "B")
+        D3(2, 0)
+        O3(2, 1, S)
+        M3(2, 3, 1)
+        O3(2, 3, S)
+        D3(2, 1)
+        O3(2, 2, V)
         D3(2, 2)
-        D2(1, 3)
-        SPS(1, 1, "A")
+        SPS(0, 1, "B")
+        SPW(1, 0, 3, "B")
+        SPS(1, 1, "B")
+        D3(2, 3)

from contextlib import ExitStack

import concourse.mybir as mybir
from concourse.masks import make_identity

F32 = mybir.dt.float32
BF16 = mybir.dt.bfloat16
U32 = mybir.dt.uint32
I32 = mybir.dt.int32
U8 = mybir.dt.uint8
FP8 = mybir.dt.float8_e4m3fn
FP8X4 = mybir.dt.float8_e4m3fn_x4
FP4X4 = mybir.dt.float4_e2m1fn_x4
MULT = mybir.AluOpType.mult
ADD = mybir.AluOpType.add
ABS = mybir.ActivationFunctionType.Abs
COPY = mybir.ActivationFunctionType.Copy

M, K, N, R, C = 1024, 1024, 1536, 512, 1024
FLOPS = 2 * (M * K * N + M * N * C + R * M * N)
P = 128
B = 512
BANKS = {"A": 4, "B": 3, "C": 1}


def tile_crystal_slip_rates_s8_kernel(
    tc, sigma, schmid_bytes, schmid_scale, rate, back_words, back_scales, mem, strain, acc
):
    nc = tc.nc
    S, V, PE, G = nc.scalar, nc.vector, nc.tensor, nc.gpsimd
    with ExitStack() as ctx:
        keep = ctx.enter_context(tc.tile_pool(name="keep", bufs=1))
        work = ctx.enter_context(tc.tile_pool(name="work", bufs=2))
        psum = ctx.enter_context(tc.psum_pool(name="psum", bufs=1))

        ident = keep.tile([P, P], F32, name="ident")
        touch = keep.tile([P, 8], F32, name="touch")
        zb = keep.tile([P, B], BF16, name="zb")
        scl = keep.tile([P, 2, 4], F32, name="scl")
        byt = keep.tile([P, 2, 4, N], U8, name="byt")
        rate_sb = keep.tile([P, 2, 4, N], BF16, name="rate_sb")
        sig_codes = keep.tile([P, 2, 2, B], U32, name="sig_codes", align_bytes=64)
        sig_sc = keep.tile([P, 2, 2, B], U8, name="sig_sc", align_bytes=64)
        sch_codes = keep.tile([P, 2, N], U32, name="sch_codes", align_bytes=64)
        sch_sc = keep.tile([P, 2, N], U8, name="sch_sc", align_bytes=64)
        mem_codes = keep.tile([P, 2, B], U32, name="mem_codes", align_bytes=64)
        mem_sc = keep.tile([P, 2, B], U8, name="mem_sc", align_bytes=64)
        row_codes = keep.tile([P, 2, N], U32, name="row_codes", align_bytes=64)
        row_sc = keep.tile([P, 2, N], U8, name="row_sc", align_bytes=64)
        col_codes = keep.tile([P, 2, 3, B], U32, name="col_codes", align_bytes=64)
        col_sc = keep.tile([P, 2, 3, B], U8, name="col_sc", align_bytes=64)
        bw = keep.tile([P, 3, 2 * C], U8, name="bw", align_bytes=64)
        bsc = keep.tile([P, 3, C], U8, name="bsc", align_bytes=64)

        V.memset(zb[:], 0.0)
        V.memset(touch[:], 0.0)
        S.activation(out=touch[:, 1:2], in_=touch[:, 0:1], func=ABS)
        make_identity(nc, ident[:])
        nc.gpsimd.memset(bsc[:].rearrange("p g n -> p (g n)").bitcast(I32), 0)

        raw = {}

        def load_rows(key, src, t0):
            raw[key] = work.tile([P, 2, 1024], BF16, name="raw", tag="raw", bufs=4, align_bytes=64)
            v = src.rearrange("(p t) k -> p t k", t=4)
            nc.sync.dma_start(out=raw[key][:], in_=v[:, t0 : t0 + 2, :])

        def load_sigma(h, t0):
            load_rows(("s", h, t0), sigma[h * B : (h + 1) * B, :], t0)

        def load_bytes(g, t):
            v = schmid_bytes[g * B : (g + 1) * B, :].rearrange("(p t) n -> p t n", t=4)
            nc.sync.dma_start(out=byt[:, g, t], in_=v[:, t, :])

        def load_rate(h, t0):
            v = rate[h * B : (h + 1) * B, :].rearrange("(p t) n -> p t n", t=4)
            nc.sync.dma_start(out=rate_sb[:, h, t0 : t0 + 2], in_=v[:, t0 : t0 + 2, :])

        def load_back():
            nc.sync.dma_start(out=bw[:].bitcast(I32), in_=back_words.rearrange("g p w -> p g w").bitcast(I32))
            for q in range(4):
                nc.sync.dma_start(
                    out=bsc[32 * q : 32 * q + 4].bitcast(I32),
                    in_=back_scales[:, 4 * q : 4 * q + 4, :].rearrange("g q n -> q g n").bitcast(I32),
                )

        def load_scale():
            nc.scalar.dma_start(out=scl[:], in_=schmid_scale.rearrange("(g p t) o -> p g (t o)", p=P, t=4))

        def copy(eng, out, in_):
            if eng is S:
                S.copy(out=out, in_=in_)
            else:
                V.tensor_copy(out=out, in_=in_)

        def weave(eng, out, in_):
            if eng is G:
                G.tensor_scalar(out=out, in0=in_.rearrange("p t c -> p c t"), scalar1=1.0, scalar2=0.0, op0=MULT, op1=ADD)
                return
            copy(eng, out.rearrange("p (c i) t -> p c t i", i=4), in_.rearrange("p t (c i) -> p c t i", i=4))

        def bank(tag, shape):
            return psum.tile(shape, F32, name="ps" + tag, tag="ps" + tag, bufs=BANKS[tag])

        def spin(src, tag):
            d = bank(tag, [P, B])
            PE.matmul(out=d[:], lhsT=src[:, 0:P], rhs=src, start=True, stop=True)

        def SPZ(tag):
            spin(zb[:], tag)

        def SPW(g, nb, t, tag):
            spin(wide[(g, nb)][:, t, :], tag)

        def SPI(g, nb, tag):
            spin(grp[("sch", g, nb)][:, 0:P, :].rearrange("p c t -> p (c t)"), tag)

        def SPS(u, t, tag):
            spin(slip[u][:, t, :], tag)

        grp, trs = {}, {}

        def turn_pe(key, src, wbase, step, tag):
            tr = bank(tag, [P, 2, 2, P])
            for a in range(2):
                words = src[:, a, :].bitcast(F32)
                for u in range(2):
                    w = words[:, wbase + u : wbase + 256 : 2] if step == 2 else words[:, u * P : (u + 1) * P]
                    PE.transpose(tr[:, a, u, :], w, ident[:])
            trs[key] = tr

        def turn_copy(key, eng):
            grp[key] = work.tile([P, 2 * P, 4], BF16, name="half", tag="half", bufs=6, align_bytes=64)
            copy(
                eng,
                grp[key][:].bitcast(F32).rearrange("p (a r) u -> p a r u", a=2),
                trs[key][:].rearrange("p a u r -> p a r u"),
            )

        def quant(key, codes, scales, c0, c1):
            V.quantize_mx(
                out=codes.bitcast(FP8X4),
                scales=scales,
                in_=grp[key][:, c0:c1, :].rearrange("p c t -> p (c t)"),
            )

        def ST(h, g, t0, tag):
            turn_pe(("s", h, g, t0), raw[("s", h, t0)], 256 * g, 2, tag)

        def SC(h, g, t0, eng):
            turn_copy(("s", h, g, t0), eng)

        def SQ(h, g, t0):
            c = slice(t0 * P, (t0 + 2) * P)
            quant(("s", h, g, t0), sig_codes[:, h, g, c], sig_sc[:, h, g, c], 0, 2 * P)

        def MT(g, t0, tag):
            turn_pe(("m", g, t0), raw[("m", t0)], 256 * g, 2, tag)

        def MC(g, t0, eng):
            turn_copy(("m", g, t0), eng)

        def MQ(g, t0):
            c = slice(t0 * P, (t0 + 2) * P)
            quant(("m", g, t0), mem_codes[:, g, c], mem_sc[:, g, c], 0, 2 * P)

        wide = {}

        def W(g, nb, t, eng):
            key = (g, nb)
            if key not in wide:
                wide[key] = work.tile([P, 4, B], BF16, name="wide", tag="wide", bufs=3, align_bytes=64)
            b = byt[:, g, t, nb * B : (nb + 1) * B]
            b = b.bitcast(FP8)
            s = scl[:, g, t : t + 1]
            if eng is S:
                S.activation(out=wide[key][:, t, :], in_=b, func=COPY, scale=s)
            else:
                V.tensor_scalar(out=wide[key][:, t, :], in0=b, scalar1=s, scalar2=None, op0=MULT)

        def new_grp(key):
            if key not in grp:
                grp[key] = work.tile([P, B, 4], BF16, name="grp", tag="grp", bufs=4, align_bytes=64)

        def I(g, nb, eng):
            key = ("sch", g, nb)
            new_grp(key)
            weave(eng, grp[key][:], wide[(g, nb)][:])

        def Q(g, nb):
            c = slice(nb * B, nb * B + B)
            quant(("sch", g, nb), sch_codes[:, g, c], sch_sc[:, g, c], 0, B)

        tau, w_sb, a_sb, slip = {}, {}, {}, {}

        def mm(out, lc, ls, rc, rs, start, stop, fp4=False):
            PE.matmul_mx(
                out=out,
                lhsT=lc.bitcast(FP8X4),
                lhsT_scale=ls,
                rhs=rc.bitcast(FP4X4 if fp4 else FP8X4),
                rhs_scale=rs,
                start=start,
                stop=stop,
            )

        units = [(0, 0), (0, 1), (0, 2), (1, 0), (1, 1), (1, 2)]

        def TA(u, t, tag):
            h, nb = units[u]
            ps = bank(tag, [P, B])
            c, n = slice(t * P, (t + 1) * P), slice(nb * B, nb * B + B)
            for g in range(2):
                mm(ps[:], sig_codes[:, h, g, c], sig_sc[:, h, g, c], sch_codes[:, g, n], sch_sc[:, g, n], g == 0, g == 1)
            tau[(u, t)] = ps

        def even_odd(cols, natural):
            if natural:
                return cols.rearrange("p (i u e) -> p u i e", u=2, e=2)
            return cols.rearrange("p (u i e) -> p u i e", u=2, e=2)

        def AB(u, t):
            k = (u, t // 2)
            if k not in a_sb:
                a_sb[k] = work.tile([P, 2, B], F32, name="a_sb", tag="a_sb", bufs=3)
            S.activation(out=even_odd(a_sb[k][:, t % 2, :], False), in_=even_odd(tau[(u, t)][:], True), func=ABS)

        def V1(u, t):
            k = (u, t // 2)
            h, nb = units[u]
            if k not in w_sb:
                w_sb[k] = work.tile([P, 2, B], F32, name="w_sb", tag="w_sb", bufs=2)
            V.tensor_tensor(
                out=even_odd(w_sb[k][:, t % 2, :], False),
                in0=even_odd(tau[(u, t)][:], True),
                in1=even_odd(rate_sb[:, h, t, nb * B : nb * B + B], True),
                op=MULT,
            )

        def PR(u, t0, eng):
            k = (u, t0 // 2)
            if u not in slip:
                slip[u] = work.tile([P, 4, B], BF16, name="slip", tag="slip", bufs=6, align_bytes=64)
            eng.tensor_tensor(out=slip[u][:, t0 : t0 + 2, :], in0=w_sb[k][:], in1=a_sb[k][:], op=MULT)

        def CT(u, t0, tag):
            turn_pe(("c", u, t0), slip[u][:, t0 : t0 + 2, :], 0, 1, tag)

        def CC(u, t0, eng):
            turn_copy(("c", u, t0), eng)

        def CQ(u, t0):
            h, nb = units[u]
            c = slice(t0 * P, (t0 + 2) * P)
            quant(("c", u, t0), col_codes[:, h, nb, c], col_sc[:, h, nb, c], 0, 2 * P)

        def RI(u, p, eng):
            key = ("r", u)
            new_grp(key)
            c = slice(*((0, 256), (256, 384), (384, 512))[p])
            weave(eng, grp[key][:, c, :], slip[u][:, :, c])

        def RQ(u, p):
            h, nb = units[u]
            c0, c1 = (0, B) if p == 2 else (256 * p, 256 * (p + 1))
            n = slice(nb * B + c0, nb * B + c1)
            quant(("r", u), row_codes[:, h, n], row_sc[:, h, n], c0, c1)

        strain_v = strain.rearrange("(h p t) c -> h p t c", p=P, t=4)
        acc_v = acc.rearrange("(p s) n -> p s n", s=4)
        st2, st3, osb = {}, {}, {}

        def M2(h, t, c, part, tag=None):
            key = (h, t, c)
            if part == 0:
                st2[key] = bank(tag, [P, B])
            m = slice(t * P, t * P + P)
            for g in (range(2) if part == 0 else (2,)):
                mm(
                    st2[key][:],
                    col_codes[:, h, g, m],
                    col_sc[:, h, g, m],
                    bw[:, g, 2 * c * B : 2 * (c + 1) * B],
                    bsc[:, g, c * B : (c + 1) * B],
                    g == 0,
                    g == 2,
                    fp4=True,
                )

        def O2(h, t, c, eng):
            if (h, t) not in osb:
                osb[(h, t)] = work.tile([P, C], F32, name="osb", tag="osb", bufs=3)
            copy(eng, osb[(h, t)][:, c * B : (c + 1) * B], st2[(h, t, c)][:])

        def D2(h, t, c):
            cols = slice(0, C) if c == 2 else slice(c * B, (c + 1) * B)
            nc.sync.dma_start(out=strain_v[h, :, t, cols], in_=osb[(h, t)][:, cols])

        def M3(nb, s, p, tag=None):
            key = (nb, s)
            if p != 1:
                st3[key] = bank(tag, [P, B])
            c0, c1 = (0, B) if p == 2 else (256 * p, 256 * (p + 1))
            m, n = slice(s * P, s * P + P), slice(nb * B + c0, nb * B + c1)
            for h in range(2):
                mm(st3[key][:, c0:c1], mem_codes[:, h, m], mem_sc[:, h, m], row_codes[:, h, n], row_sc[:, h, n], h == 0, h == 1)

        oacc = {}

        def O3(nb, s, eng):
            o = work.tile([P, B], F32, name="oacc", tag="oacc", bufs=5)
            oacc[(nb, s)] = o
            copy(
                eng,
                o[:].rearrange("p (i u e) -> p i u e", u=2, e=2),
                st3[(nb, s)][:].rearrange("p (u i e) -> p i u e", u=2, e=2),
            )

        def D3(nb, s):
            nc.sync.dma_start(out=acc_v[:, s, nb * B : nb * B + B], in_=oacc[(nb, s)][:])

        ctx.enter_context(
            tc.manual_schedule(engines={mybir.EngineType.PE, mybir.EngineType.Activation, mybir.EngineType.DVE, mybir.EngineType.SP, mybir.EngineType.Pool})
        )
        SPZ("B")
        load_bytes(0, 2)
        SPZ("B")
        SPZ("C")
        load_scale()
        W(0, 2, 2, V)
        W(0, 0, 2, V)
        SPZ("C")
        W(0, 1, 2, S)
        load_bytes(0, 0)
        W(0, 1, 0, V)
        W(0, 0, 0, S)
        W(0, 2, 0, V)
        load_bytes(0, 3)
        SPZ("B")
        W(0, 0, 3, V)
        W(0, 1, 3, S)
        SPW(0, 0, 3, "A")
        load_bytes(0, 1)
        load_sigma(0, 0)
        W(0, 2, 3, V)
        SPW(0, 0, 3, "B")
        W(0, 0, 1, V)
        W(0, 2, 1, V)
        I(0, 0, V)
        I(0, 2, V)
        W(0, 1, 1, S)
        I(0, 1, S)
        load_bytes(1, 3)
        W(1, 2, 3, V)
        load_bytes(1, 0)
        W(1, 0, 0, V)
        load_bytes(1, 2)
        W(1, 1, 2, V)
        SPZ("A")
        Q(0, 0)
        W(1, 2, 0, V)
        ST(0, 1, 0, "B")
        SC(0, 1, 0, S)
        SQ(0, 1, 0)
        W(1, 1, 3, S)
        W(1, 0, 3, V)
        Q(0, 2)
        load_bytes(1, 1)
        W(1, 0, 1, S)
        W(1, 0, 2, S)
        I(1, 0, V)
        W(1, 1, 0, S)
        ST(0, 0, 0, "B")
        load_sigma(1, 0)
        ST(1, 1, 0, "A")
        W(1, 1, 1, S)
        I(1, 1, V)
        ST(1, 0, 0, "A")
        Q(1, 0)
        SC(0, 0, 0, S)
        SQ(0, 0, 0)
        SC(1, 1, 0, S)
        SQ(1, 1, 0)
        Q(0, 1)
        SPI(1, 0, "C")
        Q(1, 1)
        load_rows(("m", 0), mem, 0)
        SC(1, 0, 0, S)
        SQ(1, 0, 0)
        SPZ("C")
        SPI(1, 0, "B")
        SPI(1, 1, "C")
        W(1, 2, 1, S)
        TA(0, 1, "A")
        load_rate(0, 0)
        V1(0, 1)
        TA(0, 0, "A")
        V1(0, 0)
        TA(1, 1, "A")
        SPI(1, 1, "B")
        V1(1, 1)
        TA(1, 0, "B")
        V1(1, 0)
        W(1, 2, 2, S)
        I(1, 2, S)
        Q(1, 2)
        AB(0, 1)
        AB(0, 0)
        PR(0, 0, V)
        AB(1, 0)
        TA(3, 1, "B")
        AB(3, 1)
        AB(1, 1)
        load_rate(1, 0)
        V1(3, 1)
        load_sigma(0, 2)
        ST(0, 0, 2, "A")
        SC(0, 0, 2, S)
        PR(1, 0, V)
        load_sigma(1, 2)
        SQ(0, 0, 2)
        ST(0, 1, 2, "A")
        SC(0, 1, 2, S)
        SQ(0, 1, 2)
        TA(3, 0, "B")
        load_rate(0, 2)
        ST(1, 0, 2, "A")
        AB(3, 0)
        V1(3, 0)
        ST(1, 1, 2, "B")
        SC(1, 1, 2, S)
        SQ(1, 1, 2)
        TA(2, 1, "A")
        TA(2, 0, "A")
        CT(0, 0, "C")
        CT(1, 0, "A")
        AB(2, 0)
        V1(2, 1)
        V1(2, 0)
        MT(0, 0, "B")
        PR(3, 0, G)
        CC(0, 0, V)
        CQ(0, 0)
        SC(1, 0, 2, S)
        AB(2, 1)
        load_rows(("m", 2), mem, 2)
        TA(1, 2, "B")
        MC(0, 0, S)
        load_back()
        AB(1, 2)
        TA(1, 3, "B")
        AB(1, 3)
        MT(0, 2, "A")
        PR(2, 0, G)
        MT(1, 2, "B")
        CC(1, 0, V)
        MC(0, 2, S)
        CT(3, 0, "C")
        CC(3, 0, S)
        V1(1, 2)
        V1(1, 3)
        TA(2, 2, "A")
        AB(2, 2)
        SPS(0, 1, "A")
        TA(2, 3, "A")
        SQ(1, 0, 2)
        PR(1, 2, V)
        TA(4, 1, "A")
        MC(1, 2, S)
        CT(2, 0, "C")
        AB(4, 1)
        V1(2, 3)
        CQ(1, 0)
        SPZ("B")
        CC(2, 0, S)
        CQ(2, 0)
        TA(4, 0, "B")
        V1(4, 0)
        V1(2, 2)
        M2(0, 0, 0, 0, "B")
        RI(1, 1, G)
        RI(1, 0, S)
        AB(2, 3)
        TA(5, 0, "B")
        AB(5, 0)
        SPS(1, 1, "C")
        CT(1, 2, "C")
        V1(4, 1)
        PR(2, 2, V)
        MT(1, 0, "A")
        AB(4, 0)
        MQ(0, 0)
        TA(5, 1, "A")
        AB(5, 1)
        V1(5, 0)
        M2(0, 0, 0, 1)
        CC(1, 2, S)
        TA(0, 3, "A")
        V1(5, 1)
        MC(1, 0, S)
        O2(0, 0, 0, V)
        RI(1, 2, G)
        TA(0, 2, "B")
        AB(0, 2)
        M2(0, 0, 1, 0, "A")
        M2(0, 0, 1, 1)
        PR(4, 0, G)
        MQ(0, 2)
        O2(0, 0, 1, V)
        AB(0, 3)
        M2(0, 1, 1, 0, "A")
        TA(3, 2, "A")
        AB(3, 2)
        V1(0, 2)
        M2(0, 1, 0, 0, "B")
        PR(5, 0, G)
        M2(0, 1, 1, 1)
        O2(0, 1, 1, S)
        TA(3, 3, "B")
        AB(3, 3)
        M2(0, 1, 0, 1)
        O2(0, 1, 0, S)
        TA(4, 2, "B")
        AB(4, 2)
        SPW(1, 0, 3, "C")
        V1(0, 3)
        load_rate(1, 2)
        CT(5, 0, "C")
        CC(5, 0, S)
        PR(0, 2, V)
        D2(0, 0, 2)
        CT(4, 0, "B")
        CQ(3, 0)
        CT(0, 2, "A")
        CC(0, 2, S)
        D2(0, 1, 2)
        MQ(1, 2)
        V1(3, 2)
        V1(3, 3)
        CT(2, 2, "A")
        CC(2, 2, S)
        RI(0, 1, G)
        CQ(0, 2)
        TA(4, 3, "A")
        TA(5, 3, "A")
        CQ(1, 2)
        M2(0, 3, 1, 0, "A")
        M2(0, 2, 0, 0, "B")
        PR(3, 2, V)
        CQ(2, 2)
        CC(4, 0, S)
        CQ(4, 0)
        M2(0, 3, 0, 0, "C")
        M2(0, 3, 0, 1)
        M2(0, 3, 1, 1)
        M2(0, 2, 0, 1)
        RI(3, 2, G)
        RI(0, 2, S)
        V1(4, 2)
        M2(0, 2, 1, 0, "B")
        RI(0, 0, S)
        O2(0, 3, 0, V)
        O2(0, 3, 1, S)
        D2(0, 3, 2)
        M2(0, 2, 1, 1)
        AB(5, 3)
        V1(4, 3)
        AB(4, 3)
        TA(5, 2, "C")
        RI(3, 0, V)
        RQ(0, 2)
        O2(0, 2, 0, S)
        CT(3, 2, "B")
        O2(0, 2, 1, S)
        D2(0, 2, 2)
        AB(5, 2)
        CC(3, 2, S)
        M2(1, 0, 0, 0, "A")
        RI(3, 1, G)
        CQ(5, 0)
        RQ(3, 2)
        M2(1, 0, 0, 1)
        M3(0, 2, 2, "B")
        O3(0, 2, S)
        MQ(1, 0)
        M3(0, 1, 2, "A")
        O2(1, 0, 0, V)
        M2(1, 0, 1, 0, "B")
        M2(1, 0, 1, 1)
        O3(0, 1, S)
        M3(0, 0, 2, "B")
        PR(4, 2, V)
        O2(1, 0, 1, S)
        D3(0, 2)
        RI(4, 2, S)
        RI(4, 0, G)
        V1(5, 2)
        M2(1, 1, 0, 0, "B")
        D3(0, 1)
        M2(1, 1, 0, 1)
        V1(5, 3)
        RI(4, 1, S)
        O2(1, 1, 0, S)
        M2(1, 1, 1, 0, "B")
        M2(1, 1, 1, 1)
        O2(1, 1, 1, S)
        M3(0, 3, 2, "A")
        D2(1, 0, 2)
        O3(0, 0, V)
        PR(5, 2, V)
        CT(5, 2, "B")
        D3(0, 0)
        RQ(1, 2)
        O3(0, 3, S)
        CT(4, 2, "A")
        CC(4, 2, S)
        RQ(4, 2)
        CC(5, 2, V)
        D2(1, 1, 2)
        M3(1, 2, 2, "A")
        M3(1, 0, 2, "A")
        O3(1, 2, S)
        O3(1, 0, S)
        M3(1, 3, 2, "A")
        CQ(4, 2)
        CQ(3, 2)
        D3(0, 3)
        D3(1, 2)
        M2(1, 3, 1, 0, "B")
        CQ(5, 2)
        M2(1, 3, 1, 1)
        RI(2, 1, G)
        O3(1, 3, V)
        D3(1, 0)
        D3(1, 3)
        RI(2, 2, S)
        RI(5, 0, G)
        RI(5, 2, S)
        O2(1, 3, 1, V)
        RI(2, 0, S)
        RI(5, 1, G)
        M2(1, 2, 0, 0, "B")
        M2(1, 2, 0, 1)
        D2(1, 3, 1)
        O2(1, 2, 0, V)
        M3(1, 1, 2, "B")
        O3(1, 1, V)
        D2(1, 2, 0)
        M2(1, 2, 1, 0, "A")
        M2(1, 2, 1, 1)
        O2(1, 2, 1, S)
        D3(1, 1)
        M2(1, 3, 0, 0, "A")
        RQ(2, 2)
        M2(1, 3, 0, 1)
        D2(1, 2, 1)
        RQ(5, 0)
        O2(1, 3, 0, S)
        RQ(5, 1)
        D2(1, 3, 0)
        M3(2, 0, 0, "A")
        M3(2, 0, 1)
        M3(2, 1, 0, "B")
        O3(2, 0, S)
        M3(2, 1, 1)
        SPZ("B")
        M3(2, 2, 0, "C")
        M3(2, 2, 1)
        M3(2, 3, 0, "B")
        D3(2, 0)
        O3(2, 1, S)
        M3(2, 3, 1)
        O3(2, 3, S)
        D3(2, 1)
        O3(2, 2, V)
        D3(2, 2)
        SPS(0, 1, "B")
        SPW(1, 0, 3, "B")
        SPS(1, 1, "B")
        D3(2, 3)
